import numpy as np
import ml_dtypes


def mxq(x, axis, fmt="e4m3"):
    dtype, down = {"e4m3": (ml_dtypes.float8_e4m3fn, 7), "e5m2": (ml_dtypes.float8_e5m2, 14)}[fmt]
    v = np.moveaxis(np.asarray(x, np.float32).astype(ml_dtypes.bfloat16).astype(np.float64), axis, -1)
    blocks = v.reshape(v.shape[:-1] + (-1, 32))
    amax = np.abs(blocks).max(-1, keepdims=True)
    byte = np.maximum(np.where(amax > 0, np.frexp(amax)[1] - 1 + 127, 0) - down, 1)
    scale = np.exp2(byte - 127.0)
    codes = (blocks / scale).astype(np.float32).astype(dtype).astype(np.float64)
    return np.moveaxis((codes * scale).reshape(v.shape), -1, axis)


WIDE = False


def mx_kscale(k):
    if not WIDE:
        return np.ones(k)
    levels = np.array([10, -10, 5, -5, 0])
    if k % 512:
        return np.exp2(np.random.permutation(np.resize(levels, k // 32))).repeat(32)
    a = np.empty((k // 512, 16))
    for p in range(k // 512):
        a[p, :8] = np.random.permutation(np.resize(levels, 8))
        for g in range(8):
            far = levels[np.abs(levels - a[p, g]) >= 10]
            a[p, g + 8] = far[np.random.randint(len(far))]
    return np.exp2(a.ravel()).repeat(32)


def f64(x):
    return np.asarray(x).astype(np.float64)


def striped(idx):
    return np.tile(idx.reshape(-1, 16).T, (8, 1)).astype(np.uint16)


def unstriped(offs):
    return offs[:16].T.reshape(-1).astype(np.int64)


K, T, E, C, N = 512, 1280, 15, 256, 128
TOP = 3


def by_expert(wq, xq):
    return np.concatenate([wq[e].T @ xq[:, e * C:(e + 1) * C] for e in range(E)], axis=1)


def setup_inputs():
    n = np.random.standard_normal
    s = mx_kscale(K)[:, None]
    deal = np.repeat(np.arange(E), C).reshape(TOP, T)[:, np.random.permutation(T)]
    deal = np.take_along_axis(deal, np.argsort(np.random.rand(TOP, T), axis=0), axis=0)
    for _ in range(8):
        s_, t_ = np.random.permutation(T).reshape(2, -1); r = np.random.randint(TOP, size=T // 2); x, y = deal[r, s_].copy(), deal[r, t_].copy()
        ok = ~((deal[:, s_] == y).any(0) | (deal[:, t_] == x).any(0)); deal[r[ok], s_[ok]] = y[ok]; deal[r[ok], t_[ok]] = x[ok]
    order = np.lexsort((np.random.rand(TOP * T), deal.reshape(-1)))
    slot_token = order % T; pos = np.empty(TOP * T, np.int64); pos[order] = np.arange(TOP * T); pos = pos.reshape(TOP, T)
    g = np.random.uniform(0.5, 1.5, (TOP, T)); g = g / g.sum(0)
    return {
        "xT": (n((K, T)) * s).astype(np.float32),
        "w": (n((E + 1, K, N)) / np.sqrt(K) / s[None]).astype(np.float32),
        "gate": np.stack([np.tile(r, (N, 1)) for r in g]).astype(np.float32),
        "offs": striped(slot_token),
        "pos1": striped(pos[0]),
        "pos2": striped(pos[1]),
        "pos3": striped(pos[2]),
    }


def reference(xT, w, gate, offs, pos1, pos2, pos3):
    idx = unstriped(offs)
    wq = mxq(f64(w), 1, "e4m3")
    xs = mxq(f64(xT), 0, "e4m3")
    ys = wq[E].T @ xs
    xq = mxq(f64(xT)[:, idx], 0, "e4m3")
    y = by_expert(wq, xq)
    return ys + sum(f64(gate[r]) * y[:, unstriped(p)] for r, p in enumerate((pos1, pos2, pos3)))

@@ -1,0 +1,206 @@
+from contextlib import ExitStack
+
+import concourse.mybir as mybir
+from concourse.masks import make_identity
+
+K, T, E, C, N = 512, 1280, 15, 256, 128
+SLOTS = E * C
+FLOPS = 2 * K * N * (SLOTS + T)
+
+F32 = mybir.dt.float32
+BF16 = mybir.dt.bfloat16
+U32 = mybir.dt.uint32
+U16 = mybir.dt.uint16
+U8 = mybir.dt.uint8
+FP8X4 = mybir.dt.float8_e4m3fn_x4
+MULT = mybir.AluOpType.mult
+ADD = mybir.AluOpType.add
+
+P = 128
+PACK = 4
+STRIPE = 16
+BANK = 512
+BANKS = 8
+X_CHUNKS = [(0, 512), (512, 1024), (1024, 1280)]
+GROUPS = [(s, min(s + BANK, SLOTS)) for s in range(0, SLOTS, BANK)]
+SHARED = [(s, min(s + BANK, T)) for s in range(0, T, BANK)]
+OUT_CHUNKS = [(0, 256), (256, 512), (512, 768), (768, 1024), (1024, 1152), (1152, 1280)]
+PICKED = 3
+GROUPED = 3
+WEIGHTS_AHEAD = 2
+COLLECT_BEHIND = 3
+
+
+def tile_moe_shr_lin_none_kernel(tc, xT, w, gate, offs, pos1, pos2, pos3, out):
+    nc = tc.nc
+    with ExitStack() as ctx:
+        keep = ctx.enter_context(tc.tile_pool(name="keep", bufs=1))
+        psum = ctx.enter_context(tc.psum_pool(name="psum", bufs=1))
+
+        x_rows = xT.rearrange("(p h j) t -> p h j t", h=2, j=2)
+        x_raw = {}
+        offsets = keep.tile([P, SLOTS // STRIPE], U16, name="offsets")
+        for h in range(2):
+            for a, b in X_CHUNKS:
+                x_raw[h, a] = keep.tile([P, 2, b - a], F32, name="x_raw_%d_%d" % (h, a))
+                nc.sync.dma_start(x_raw[h, a][:], x_rows[:, h, :, a:b])
+            if h == 0:
+                nc.sync.dma_start(offsets[:], offs)
+        w_raw = []
+        for g in range(len(GROUPS)):
+            w_raw.append(keep.tile([P, 2, PACK, N], F32, name="w_raw_%d" % g))
+            nc.sync.dma_start(w_raw[g][:], w[2 * g : 2 * g + 2].rearrange("e (p j) n -> p e j n", j=PACK))
+        places = []
+        gates = []
+        for r, pos in enumerate((pos1, pos2, pos3)):
+            places.append(keep.tile([P, T // STRIPE], U16, name="places_%d" % r))
+            nc.sync.dma_start(places[r][:], pos)
+        for r in range(3):
+            gates.append(keep.tile([P, T], F32, name="gates_%d" % r))
+            nc.sync.dma_start(gates[r][:], gate[r])
+
+        identity = keep.tile([P, P], F32, name="identity")
+        make_identity(nc, identity[:])
+
+        x_pairs = keep.tile([P, 2, T, 2], BF16, name="x_pairs", align_bytes=64)
+        for a, b in X_CHUNKS:
+            nc.vector.tensor_copy(x_pairs[:, 0, a:b, :], x_raw[0, a][:].rearrange("p j t -> p t j"))
+        for a, b in X_CHUNKS:
+            nc.scalar.copy(x_pairs[:, 1, a:b, :], x_raw[1, a][:].rearrange("p j t -> p t j"))
+        x_words = x_pairs[:].rearrange("p h t j -> p (h t j)").bitcast(U32)
+
+        banks = [psum.tile([P, BANK], F32, name="bank_%d" % i) for i in range(BANKS)]
+        picked = [keep.tile([P, 2 * BANK], U32, name="picked_%d" % i, align_bytes=64) for i in range(PICKED)]
+        grouped = [keep.tile([P, 2 * BANK], F32, name="grouped_%d" % i, align_bytes=64) for i in range(GROUPED)]
+        codes = [keep.tile([P, BANK], U32, name="codes_%d" % i, align_bytes=64) for i in range(GROUPED)]
+        scales = [keep.tile([P, BANK], U8, name="scales_%d" % i, align_bytes=64) for i in range(GROUPED)]
+        w_grouped = keep.tile([P, E + 1, N, PACK], BF16, name="w_grouped", align_bytes=64)
+        w_codes = keep.tile([P, (E + 1) * N], U32, name="w_codes", align_bytes=64)
+        w_scales = keep.tile([P, (E + 1) * N], U8, name="w_scales", align_bytes=64)
+        y = keep.tile([P, SLOTS], F32, name="y")
+        ys = keep.tile([P, T], F32, name="ys")
+
+        def gather(g, h):
+            a, b = GROUPS[g]
+            window = x_words[:, h * T : (h + 1) * T]
+            nc.vector.tensor_copy(
+                picked[g % PICKED][:, h * BANK : h * BANK + b - a],
+                window.indirect(offsets[:, a // STRIPE : b // STRIPE]),
+            )
+
+        def interleave(g):
+            a, b = GROUPS[g]
+            nc.scalar.copy(
+                grouped[g % GROUPED][:, : 2 * (b - a)].rearrange("p (s h) -> p s h", h=2),
+                picked[g % PICKED][:].bitcast(F32).rearrange("p (h s) -> p s h", h=2)[:, : b - a, :],
+            )
+
+        def round_weights(g):
+            for e in range(2):
+                nc.scalar.copy(
+                    w_grouped[:, 2 * g + e].rearrange("p (c i) j -> p c j i", i=4),
+                    w_raw[g][:, e].rearrange("p j (c i) -> p c j i", i=4),
+                )
+
+        def quantize_weights(g):
+            cols = slice(2 * g * N, (2 * g + 2) * N)
+            nc.vector.quantize_mx(
+                out=w_codes[:, cols].bitcast(FP8X4),
+                scales=w_scales[:, cols],
+                in_=w_grouped[:, 2 * g : 2 * g + 2].rearrange("p e n j -> p (e n j)"),
+            )
+
+        def quantize_columns(i, source, width):
+            nc.vector.quantize_mx(
+                out=codes[i % GROUPED][:, :width].bitcast(FP8X4),
+                scales=scales[i % GROUPED][:, :width],
+                in_=source[:, : 2 * width].bitcast(BF16),
+            )
+
+        def multiply(acc, e, i, cols):
+            w_cols = slice(e * N, (e + 1) * N)
+            nc.tensor.matmul_mx(
+                out=acc,
+                lhsT=w_codes[:, w_cols].bitcast(FP8X4),
+                lhsT_scale=w_scales[:, w_cols],
+                rhs=codes[i % GROUPED][:, cols].bitcast(FP8X4),
+                rhs_scale=scales[i % GROUPED][:, cols],
+                start=True,
+                stop=True,
+            )
+
+        def experts(g):
+            a, b = GROUPS[g]
+            quantize_columns(g, grouped[g % GROUPED], b - a)
+            for e in range(a // C, b // C):
+                cols = slice(e * C - a, (e + 1) * C - a)
+                multiply(banks[g][:, cols], e, g, cols)
+
+        def collect(g):
+            a, b = GROUPS[g]
+            nc.scalar.copy(y[:, a:b], banks[g][:, : b - a])
+
+        count = len(GROUPS)
+        for g in range(PICKED):
+            gather(g, 0)
+        for g in range(PICKED):
+            gather(g, 1)
+        for g in range(WEIGHTS_AHEAD):
+            round_weights(g)
+            quantize_weights(g)
+        for g in range(count + COLLECT_BEHIND):
+            if g < count:
+                interleave(g)
+            if g + PICKED < count:
+                gather(g + PICKED, 0)
+                gather(g + PICKED, 1)
+            if g < count:
+                experts(g)
+            if g + WEIGHTS_AHEAD < count:
+                round_weights(g + WEIGHTS_AHEAD)
+                quantize_weights(g + WEIGHTS_AHEAD)
+            if g >= COLLECT_BEHIND:
+                collect(g - COLLECT_BEHIND)
+
+        x_halves = x_words.bitcast(F32).rearrange("p (h t) -> p t h", h=2)
+        for s, (a, b) in enumerate(SHARED):
+            if s < 2:
+                side_by_side = picked[(6 + s) % PICKED][:].bitcast(F32)
+                nc.vector.tensor_copy(side_by_side[:, : 2 * (b - a)].rearrange("p (t h) -> p t h", h=2), x_halves[:, a:b, :])
+            else:
+                side_by_side = grouped[(count + s) % GROUPED][:]
+                nc.scalar.copy(side_by_side[:, : 2 * (b - a)].rearrange("p (t h) -> p t h", h=2), x_halves[:, a:b, :])
+            quantize_columns(count + s, side_by_side, b - a)
+            multiply(banks[s][:, : b - a], E, count + s, slice(0, b - a))
+            nc.scalar.copy(ys[:, a:b], banks[s][:, : b - a])
+
+        for c, (a, b) in enumerate(OUT_CHUNKS):
+            terms = [ys[:, a:b]]
+            for r in range(3):
+                term = keep.tile([P, b - a], F32, name="term_%d_%d" % (a, r))
+                nc.vector.tensor_tensor(
+                    term[:], y[:].indirect(places[r][:, a // STRIPE : b // STRIPE]), gates[r][:, a:b], MULT
+                )
+                terms.append(term[:])
+            total = keep.tile([P, b - a], F32, name="total_%d" % a)
+            if c >= len(OUT_CHUNKS) - 1:
+                first = keep.tile([P, b - a], F32, name="first_%d" % a)
+                second = keep.tile([P, b - a], F32, name="second_%d" % a)
+                nc.vector.tensor_tensor(first[:], terms[0], terms[1], ADD)
+                nc.vector.tensor_tensor(second[:], first[:], terms[2], ADD)
+                nc.vector.tensor_tensor(total[:], second[:], terms[3], ADD)
+            else:
+                turned_bank = banks[3 + (2 * c) % 4]
+                back_bank = banks[3 + (2 * c + 1) % 4]
+                turned = keep.tile([P, b - a], F32, name="turned_%d" % a)
+                blocks = [slice(i, i + P) for i in range(0, b - a, P)]
+                for block in blocks:
+                    for r, term in enumerate(terms):
+                        nc.tensor.matmul(
+                            turned_bank[:, block], term[:, block], identity[:], start=r == 0, stop=r == 3, is_transpose=True
+                        )
+                nc.scalar.copy(turned[:], turned_bank[:, : b - a])
+                for block in blocks:
+                    nc.tensor.transpose(back_bank[:, block], turned[:, block], identity[:])
+                nc.scalar.copy(total[:], back_bank[:, : b - a])
+            nc.sync.dma_start(out[:, a:b], total[:])

@@ -15,6 +15,7 @@ U8 = mybir.dt.uint8
 FP8X4 = mybir.dt.float8_e4m3fn_x4
 MULT = mybir.AluOpType.mult
 ADD = mybir.AluOpType.add
+COPY = mybir.ActivationFunctionType.Copy
 
 P = 128
 PACK = 4
@@ -24,15 +25,17 @@ BANKS = 8
 X_CHUNKS = [(0, 512), (512, 1024), (1024, 1280)]
 GROUPS = [(s, min(s + BANK, SLOTS)) for s in range(0, SLOTS, BANK)]
 SHARED = [(s, min(s + BANK, T)) for s in range(0, T, BANK)]
-OUT_CHUNKS = [(0, 256), (256, 512), (512, 768), (768, 1024), (1024, 1152), (1152, 1280)]
-PICKED = 3
-GROUPED = 3
-WEIGHTS_AHEAD = 2
-COLLECT_BEHIND = 3
+OUT_CHUNKS = [(0, 256), (256, 512), (512, 768), (768, 1024), (1024, 1152)]
+LAST_CHUNK = (1152, 1280)
+CODES = 4
+SCALAR_EXPERTS = 4
+SCALAR_WEIGHTS = [7]
+WEIGHT_ORDER = [0, 1, 7, 2, 3, 4, 5, 6]
 
 
 def tile_moe_shr_lin_none_kernel(tc, xT, w, gate, offs, pos1, pos2, pos3, out):
     nc = tc.nc
+    count = len(GROUPS)
     with ExitStack() as ctx:
         keep = ctx.enter_context(tc.tile_pool(name="keep", bufs=1))
         psum = ctx.enter_context(tc.psum_pool(name="psum", bufs=1))
@@ -46,9 +49,9 @@ def tile_moe_shr_lin_none_kernel(tc, xT, w, gate, offs, pos1, pos2, pos3, out):
                 nc.sync.dma_start(x_raw[h, a][:], x_rows[:, h, :, a:b])
             if h == 0:
                 nc.sync.dma_start(offsets[:], offs)
-        w_raw = []
-        for g in range(len(GROUPS)):
-            w_raw.append(keep.tile([P, 2, PACK, N], F32, name="w_raw_%d" % g))
+        w_raw = {}
+        for g in WEIGHT_ORDER:
+            w_raw[g] = keep.tile([P, 2, PACK, N], F32, name="w_raw_%d" % g)
             nc.sync.dma_start(w_raw[g][:], w[2 * g : 2 * g + 2].rearrange("e (p j) n -> p e j n", j=PACK))
         places = []
         gates = []
@@ -63,43 +66,62 @@ def tile_moe_shr_lin_none_kernel(tc, xT, w, gate, offs, pos1, pos2, pos3, out):
         make_identity(nc, identity[:])
 
         x_pairs = keep.tile([P, 2, T, 2], BF16, name="x_pairs", align_bytes=64)
+        x_planes = [keep.tile([P, T], BF16, name="x_plane_%d" % j) for j in range(2)]
         for a, b in X_CHUNKS:
             nc.vector.tensor_copy(x_pairs[:, 0, a:b, :], x_raw[0, a][:].rearrange("p j t -> p t j"))
+            for j in range(2):
+                nc.scalar.copy(x_planes[j][:, a:b], x_raw[0, a][:, j, :])
         for a, b in X_CHUNKS:
-            nc.scalar.copy(x_pairs[:, 1, a:b, :], x_raw[1, a][:].rearrange("p j t -> p t j"))
+            nc.gpsimd.tensor_scalar(
+                x_pairs[:, 1, a:b, :], x_raw[1, a][:].rearrange("p j t -> p t j"), 1.0, 0.0, MULT, ADD
+            )
         x_words = x_pairs[:].rearrange("p h t j -> p (h t j)").bitcast(U32)
+        x_halves = x_words.bitcast(F32).rearrange("p (h t) -> p t h", h=2)
 
         banks = [psum.tile([P, BANK], F32, name="bank_%d" % i) for i in range(BANKS)]
-        picked = [keep.tile([P, 2 * BANK], U32, name="picked_%d" % i, align_bytes=64) for i in range(PICKED)]
-        grouped = [keep.tile([P, 2 * BANK], F32, name="grouped_%d" % i, align_bytes=64) for i in range(GROUPED)]
-        codes = [keep.tile([P, BANK], U32, name="codes_%d" % i, align_bytes=64) for i in range(GROUPED)]
-        scales = [keep.tile([P, BANK], U8, name="scales_%d" % i, align_bytes=64) for i in range(GROUPED)]
+        picked = [keep.tile([P, 2 * BANK], U32, name="picked_%d" % i, align_bytes=64) for i in range(count)]
+        grouped = [keep.tile([P, 2 * BANK], F32, name="grouped_%d" % i, align_bytes=64) for i in range(count)]
+        codes = [keep.tile([P, BANK], U32, name="codes_%d" % i, align_bytes=64) for i in range(CODES)]
+        scales = [keep.tile([P, BANK], U8, name="scales_%d" % i, align_bytes=64) for i in range(CODES)]
         w_grouped = keep.tile([P, E + 1, N, PACK], BF16, name="w_grouped", align_bytes=64)
         w_codes = keep.tile([P, (E + 1) * N], U32, name="w_codes", align_bytes=64)
         w_scales = keep.tile([P, (E + 1) * N], U8, name="w_scales", align_bytes=64)
         y = keep.tile([P, SLOTS], F32, name="y")
         ys = keep.tile([P, T], F32, name="ys")
 
-        def gather(g, h):
+        def gather_words(h, g, start):
             a, b = GROUPS[g]
-            window = x_words[:, h * T : (h + 1) * T]
             nc.vector.tensor_copy(
-                picked[g % PICKED][:, h * BANK : h * BANK + b - a],
-                window.indirect(offsets[:, a // STRIPE : b // STRIPE]),
+                picked[g][:, h * BANK + start - a : h * BANK + b - a],
+                x_words[:, h * T : (h + 1) * T].indirect(offsets[:, start // STRIPE : b // STRIPE]),
+            )
+
+        def gather_values(e, j):
+            g, first = divmod(e * C, BANK)
+            pairs = picked[g][:, :BANK].bitcast(BF16).rearrange("p (s j) -> p s j", j=2)
+            nc.scalar.activation(
+                pairs[:, first : first + C, j],
+                x_planes[j][:].indirect(offsets[:, e * C // STRIPE : (e + 1) * C // STRIPE]),
+                COPY,
             )
 
         def interleave(g):
             a, b = GROUPS[g]
             nc.scalar.copy(
-                grouped[g % GROUPED][:, : 2 * (b - a)].rearrange("p (s h) -> p s h", h=2),
-                picked[g % PICKED][:].bitcast(F32).rearrange("p (h s) -> p s h", h=2)[:, : b - a, :],
+                grouped[g][:, : 2 * (b - a)].rearrange("p (s h) -> p s h", h=2),
+                picked[g][:].bitcast(F32).rearrange("p (h s) -> p s h", h=2)[:, : b - a, :],
             )
 
         def round_weights(g):
-            for e in range(2):
-                nc.scalar.copy(
-                    w_grouped[:, 2 * g + e].rearrange("p (c i) j -> p c j i", i=4),
-                    w_raw[g][:, e].rearrange("p j (c i) -> p c j i", i=4),
+            if g in SCALAR_WEIGHTS:
+                for e in range(2):
+                    nc.scalar.copy(
+                        w_grouped[:, 2 * g + e].rearrange("p (c i) j -> p c j i", i=4),
+                        w_raw[g][:, e].rearrange("p j (c i) -> p c j i", i=4),
+                    )
+            else:
+                nc.gpsimd.tensor_scalar(
+                    w_grouped[:, 2 * g : 2 * g + 2], w_raw[g][:].rearrange("p e j n -> p e n j"), 1.0, 0.0, MULT, ADD
                 )
 
         def quantize_weights(g):
@@ -112,8 +134,8 @@ def tile_moe_shr_lin_none_kernel(tc, xT, w, gate, offs, pos1, pos2, pos3, out):
 
         def quantize_columns(i, source, width):
             nc.vector.quantize_mx(
-                out=codes[i % GROUPED][:, :width].bitcast(FP8X4),
-                scales=scales[i % GROUPED][:, :width],
+                out=codes[i % CODES][:, :width].bitcast(FP8X4),
+                scales=scales[i % CODES][:, :width],
                 in_=source[:, : 2 * width].bitcast(BF16),
             )
 
@@ -123,84 +145,85 @@ def tile_moe_shr_lin_none_kernel(tc, xT, w, gate, offs, pos1, pos2, pos3, out):
                 out=acc,
                 lhsT=w_codes[:, w_cols].bitcast(FP8X4),
                 lhsT_scale=w_scales[:, w_cols],
-                rhs=codes[i % GROUPED][:, cols].bitcast(FP8X4),
-                rhs_scale=scales[i % GROUPED][:, cols],
+                rhs=codes[i % CODES][:, cols].bitcast(FP8X4),
+                rhs_scale=scales[i % CODES][:, cols],
                 start=True,
                 stop=True,
             )
 
         def experts(g):
             a, b = GROUPS[g]
-            quantize_columns(g, grouped[g % GROUPED], b - a)
+            quantize_columns(g, grouped[g], b - a)
             for e in range(a // C, b // C):
                 cols = slice(e * C - a, (e + 1) * C - a)
                 multiply(banks[g][:, cols], e, g, cols)
-
-        def collect(g):
-            a, b = GROUPS[g]
             nc.scalar.copy(y[:, a:b], banks[g][:, : b - a])
 
-        count = len(GROUPS)
-        for g in range(PICKED):
-            gather(g, 0)
-        for g in range(PICKED):
-            gather(g, 1)
-        for g in range(WEIGHTS_AHEAD):
-            round_weights(g)
-            quantize_weights(g)
-        for g in range(count + COLLECT_BEHIND):
-            if g < count:
-                interleave(g)
-            if g + PICKED < count:
-                gather(g + PICKED, 0)
-                gather(g + PICKED, 1)
-            if g < count:
-                experts(g)
-            if g + WEIGHTS_AHEAD < count:
-                round_weights(g + WEIGHTS_AHEAD)
-                quantize_weights(g + WEIGHTS_AHEAD)
-            if g >= COLLECT_BEHIND:
-                collect(g - COLLECT_BEHIND)
-
-        x_halves = x_words.bitcast(F32).rearrange("p (h t) -> p t h", h=2)
-        for s, (a, b) in enumerate(SHARED):
-            if s < 2:
-                side_by_side = picked[(6 + s) % PICKED][:].bitcast(F32)
-                nc.vector.tensor_copy(side_by_side[:, : 2 * (b - a)].rearrange("p (t h) -> p t h", h=2), x_halves[:, a:b, :])
+        def lay_tokens(s):
+            a, b = SHARED[s]
+            rows = picked[(0 + s) % count][:, : 2 * (b - a)].bitcast(F32)
+            if s < 0:
+                nc.vector.tensor_copy(rows.rearrange("p (t h) -> p t h", h=2), x_halves[:, a:b, :])
             else:
-                side_by_side = grouped[(count + s) % GROUPED][:]
-                nc.scalar.copy(side_by_side[:, : 2 * (b - a)].rearrange("p (t h) -> p t h", h=2), x_halves[:, a:b, :])
-            quantize_columns(count + s, side_by_side, b - a)
+                nc.scalar.copy(rows.rearrange("p (t h) -> p t h", h=2), x_halves[:, a:b, :])
+            return rows
+
+        def shared_expert(s, rows):
+            a, b = SHARED[s]
+            quantize_columns(count + s, rows, b - a)
             multiply(banks[s][:, : b - a], E, count + s, slice(0, b - a))
             nc.scalar.copy(ys[:, a:b], banks[s][:, : b - a])
 
+        def fetch(r, a, b):
+            term = keep.tile([P, b - a], F32, name="term_%d_%d" % (a, r))
+            nc.vector.tensor_tensor(
+                term[:], y[:].indirect(places[r][:, a // STRIPE : b // STRIPE]), gates[r][:, a:b], MULT
+            )
+            return term[:]
+
+        for j in range(2):
+            for e in range(SCALAR_EXPERTS):
+                gather_values(e, j)
+        for g, (a, b) in enumerate(GROUPS):
+            if b > SCALAR_EXPERTS * C:
+                gather_words(0, g, max(a, SCALAR_EXPERTS * C))
+        for g, (a, b) in enumerate(GROUPS):
+            gather_words(1, g, a)
+        for g in WEIGHT_ORDER:
+            round_weights(g)
+        for g in range(count):
+            interleave(g)
+        rows = [lay_tokens(s) for s in range(len(SHARED))]
+        for g in range(count):
+            quantize_weights(g)
+            experts(g)
+        for s in range(len(SHARED)):
+            shared_expert(s, rows[s])
+
         for c, (a, b) in enumerate(OUT_CHUNKS):
-            terms = [ys[:, a:b]]
-            for r in range(3):
-                term = keep.tile([P, b - a], F32, name="term_%d_%d" % (a, r))
-                nc.vector.tensor_tensor(
-                    term[:], y[:].indirect(places[r][:, a // STRIPE : b // STRIPE]), gates[r][:, a:b], MULT
-                )
-                terms.append(term[:])
+            terms = [fetch(r, a, b) for r in range(3)] + [ys[:, a:b]]
+            turned_bank = banks[3 + (2 * c) % 4]
+            back_bank = banks[3 + (2 * c + 1) % 4]
+            turned = keep.tile([P, b - a], F32, name="turned_%d" % a)
             total = keep.tile([P, b - a], F32, name="total_%d" % a)
-            if c >= len(OUT_CHUNKS) - 1:
-                first = keep.tile([P, b - a], F32, name="first_%d" % a)
-                second = keep.tile([P, b - a], F32, name="second_%d" % a)
-                nc.vector.tensor_tensor(first[:], terms[0], terms[1], ADD)
-                nc.vector.tensor_tensor(second[:], first[:], terms[2], ADD)
-                nc.vector.tensor_tensor(total[:], second[:], terms[3], ADD)
-            else:
-                turned_bank = banks[3 + (2 * c) % 4]
-                back_bank = banks[3 + (2 * c + 1) % 4]
-                turned = keep.tile([P, b - a], F32, name="turned_%d" % a)
-                blocks = [slice(i, i + P) for i in range(0, b - a, P)]
-                for block in blocks:
-                    for r, term in enumerate(terms):
-                        nc.tensor.matmul(
-                            turned_bank[:, block], term[:, block], identity[:], start=r == 0, stop=r == 3, is_transpose=True
-                        )
-                nc.scalar.copy(turned[:], turned_bank[:, : b - a])
-                for block in blocks:
-                    nc.tensor.transpose(back_bank[:, block], turned[:, block], identity[:])
-                nc.scalar.copy(total[:], back_bank[:, : b - a])
-            nc.sync.dma_start(out[:, a:b], total[:])
+            blocks = [slice(i, i + P) for i in range(0, b - a, P)]
+            for block in blocks:
+                for r, term in enumerate(terms):
+                    nc.tensor.matmul(
+                        turned_bank[:, block], term[:, block], identity[:], start=r == 0, stop=r == 3, is_transpose=True
+                    )
+            nc.scalar.copy(turned[:], turned_bank[:, : b - a])
+            for block in blocks:
+                nc.tensor.transpose(back_bank[:, block], turned[:, block], identity[:])
+            nc.scalar.copy(total[:], back_bank[:, : b - a])
+            nc.scalar.dma_start(out[:, a:b], total[:])
+
+        a, b = LAST_CHUNK
+        terms = [fetch(r, a, b) for r in range(3)]
+        first = keep.tile([P, b - a], F32, name="first")
+        second = keep.tile([P, b - a], F32, name="second")
+        total = keep.tile([P, b - a], F32, name="total_%d" % a)
+        nc.vector.tensor_tensor(first[:], ys[:, a:b], terms[0], ADD)
+        nc.vector.tensor_tensor(second[:], terms[1], terms[2], ADD)
+        nc.vector.tensor_tensor(total[:], first[:], second[:], ADD)
+        nc.sync.dma_start(out[:, a:b], total[:])

@@ -25,12 +25,12 @@ BANKS = 8
 X_CHUNKS = [(0, 512), (512, 1024), (1024, 1280)]
 GROUPS = [(s, min(s + BANK, SLOTS)) for s in range(0, SLOTS, BANK)]
 SHARED = [(s, min(s + BANK, T)) for s in range(0, T, BANK)]
-OUT_CHUNKS = [(0, 256), (256, 512), (512, 768), (768, 1024), (1024, 1152)]
-LAST_CHUNK = (1152, 1280)
+OUT_CHUNKS = [(0, 256), (256, 512), (512, 768), (768, 896), (896, 1024)]
+LAST_CHUNK = (1024, 1280)
 CODES = 4
 SCALAR_EXPERTS = 4
-SCALAR_WEIGHTS = [7]
-WEIGHT_ORDER = [0, 1, 7, 2, 3, 4, 5, 6]
+SCALAR_WEIGHTS = [0, 1]
+WEIGHT_ORDER = [2, 0, 3, 1, 4, 5, 6, 7]
 
 
 def tile_moe_shr_lin_none_kernel(tc, xT, w, gate, offs, pos1, pos2, pos3, out):
@@ -161,8 +161,8 @@ def tile_moe_shr_lin_none_kernel(tc, xT, w, gate, offs, pos1, pos2, pos3, out):
 
         def lay_tokens(s):
             a, b = SHARED[s]
-            rows = picked[(0 + s) % count][:, : 2 * (b - a)].bitcast(F32)
-            if s < 0:
+            rows = picked[(7 + s) % count][:, : 2 * (b - a)].bitcast(F32)
+            if s < 1:
                 nc.vector.tensor_copy(rows.rearrange("p (t h) -> p t h", h=2), x_halves[:, a:b, :])
             else:
                 nc.scalar.copy(rows.rearrange("p (t h) -> p t h", h=2), x_halves[:, a:b, :])
@@ -200,12 +200,13 @@ def tile_moe_shr_lin_none_kernel(tc, xT, w, gate, offs, pos1, pos2, pos3, out):
         for s in range(len(SHARED)):
             shared_expert(s, rows[s])
 
+        result = keep.tile([P, T], F32, name="result")
         for c, (a, b) in enumerate(OUT_CHUNKS):
-            terms = [fetch(r, a, b) for r in range(3)] + [ys[:, a:b]]
+            terms = [ys[:, a:b]] + [fetch(r, a, b) for r in range(3)]
             turned_bank = banks[3 + (2 * c) % 4]
             back_bank = banks[3 + (2 * c + 1) % 4]
             turned = keep.tile([P, b - a], F32, name="turned_%d" % a)
-            total = keep.tile([P, b - a], F32, name="total_%d" % a)
+            total = result[:, a:b]
             blocks = [slice(i, i + P) for i in range(0, b - a, P)]
             for block in blocks:
                 for r, term in enumerate(terms):
@@ -215,15 +216,15 @@ def tile_moe_shr_lin_none_kernel(tc, xT, w, gate, offs, pos1, pos2, pos3, out):
             nc.scalar.copy(turned[:], turned_bank[:, : b - a])
             for block in blocks:
                 nc.tensor.transpose(back_bank[:, block], turned[:, block], identity[:])
-            nc.scalar.copy(total[:], back_bank[:, : b - a])
-            nc.scalar.dma_start(out[:, a:b], total[:])
+            nc.scalar.copy(total, back_bank[:, : b - a])
+            if c + 1 < len(OUT_CHUNKS):
+                nc.sync.dma_start(out[:, a:b], total)
 
         a, b = LAST_CHUNK
         terms = [fetch(r, a, b) for r in range(3)]
         first = keep.tile([P, b - a], F32, name="first")
         second = keep.tile([P, b - a], F32, name="second")
-        total = keep.tile([P, b - a], F32, name="total_%d" % a)
         nc.vector.tensor_tensor(first[:], ys[:, a:b], terms[0], ADD)
         nc.vector.tensor_tensor(second[:], terms[1], terms[2], ADD)
-        nc.vector.tensor_tensor(total[:], first[:], second[:], ADD)
-        nc.sync.dma_start(out[:, a:b], total[:])
+        nc.vector.tensor_tensor(result[:, a:b], first[:], second[:], ADD)
+        nc.sync.dma_start(out[:, OUT_CHUNKS[-1][0] :], result[:, OUT_CHUNKS[-1][0] :])

@@ -25,10 +25,11 @@ BANKS = 8
 X_CHUNKS = [(0, 512), (512, 1024), (1024, 1280)]
 GROUPS = [(s, min(s + BANK, SLOTS)) for s in range(0, SLOTS, BANK)]
 SHARED = [(s, min(s + BANK, T)) for s in range(0, T, BANK)]
-OUT_CHUNKS = [(0, 256), (256, 512), (512, 768), (768, 896), (896, 1024)]
-LAST_CHUNK = (1024, 1280)
+OUT_CHUNKS = [(384, 640), (640, 896), (896, 1152), (1152, 1280)]
+LAST_CHUNK = (0, 384)
+LAST_PIECES = [(0, 256), (256, 384)]
 CODES = 4
-SCALAR_EXPERTS = 4
+SCALAR_EXPERTS = 5
 SCALAR_WEIGHTS = [0, 1]
 WEIGHT_ORDER = [2, 0, 3, 1, 4, 5, 6, 7]
 
@@ -201,30 +202,36 @@ def tile_moe_shr_lin_none_kernel(tc, xT, w, gate, offs, pos1, pos2, pos3, out):
             shared_expert(s, rows[s])
 
         result = keep.tile([P, T], F32, name="result")
-        for c, (a, b) in enumerate(OUT_CHUNKS):
-            terms = [ys[:, a:b]] + [fetch(r, a, b) for r in range(3)]
-            turned_bank = banks[3 + (2 * c) % 4]
-            back_bank = banks[3 + (2 * c + 1) % 4]
+
+        def add_on_tensor(c, a, b, terms, total):
+            back_bank = banks[c % 3]
+            sums = banks[3:6] if c % 2 == 0 else banks[6:8]
             turned = keep.tile([P, b - a], F32, name="turned_%d" % a)
-            total = result[:, a:b]
             blocks = [slice(i, i + P) for i in range(0, b - a, P)]
-            for block in blocks:
-                for r, term in enumerate(terms):
+            for r, term in enumerate(terms):
+                for i, block in enumerate(blocks):
                     nc.tensor.matmul(
-                        turned_bank[:, block], term[:, block], identity[:], start=r == 0, stop=r == 3, is_transpose=True
+                        sums[i][:, :P],
+                        term[:, block],
+                        identity[:],
+                        start=r == 0,
+                        stop=r == len(terms) - 1,
+                        is_transpose=True,
                     )
-            nc.scalar.copy(turned[:], turned_bank[:, : b - a])
+            for i, block in enumerate(blocks):
+                nc.scalar.copy(turned[:, block], sums[i][:, :P])
             for block in blocks:
                 nc.tensor.transpose(back_bank[:, block], turned[:, block], identity[:])
             nc.scalar.copy(total, back_bank[:, : b - a])
-            if c + 1 < len(OUT_CHUNKS):
-                nc.sync.dma_start(out[:, a:b], total)
 
         a, b = LAST_CHUNK
-        terms = [fetch(r, a, b) for r in range(3)]
-        first = keep.tile([P, b - a], F32, name="first")
-        second = keep.tile([P, b - a], F32, name="second")
-        nc.vector.tensor_tensor(first[:], ys[:, a:b], terms[0], ADD)
-        nc.vector.tensor_tensor(second[:], terms[1], terms[2], ADD)
-        nc.vector.tensor_tensor(result[:, a:b], first[:], second[:], ADD)
-        nc.sync.dma_start(out[:, OUT_CHUNKS[-1][0] :], result[:, OUT_CHUNKS[-1][0] :])
+        partial = keep.tile([P, b - a], F32, name="partial")
+        add_on_tensor(0, a, b, [ys[:, a:b]] + [fetch(r, a, b) for r in range(2)], partial[:])
+        for c, (a, b) in enumerate(OUT_CHUNKS):
+            add_on_tensor(c + 1, a, b, [ys[:, a:b]] + [fetch(r, a, b) for r in range(3)], result[:, a:b])
+            nc.scalar.dma_start(out[:, a:b], result[:, a:b])
+        base = LAST_CHUNK[0]
+        last = [fetch(2, a, b) for a, b in LAST_PIECES]
+        for (a, b), term in zip(LAST_PIECES, last):
+            nc.vector.tensor_tensor(result[:, a:b], partial[:, a - base : b - base], term, ADD)
+            nc.sync.dma_start(out[:, a:b], result[:, a:b])

@@ -29,7 +29,7 @@ OUT_CHUNKS = [(384, 640), (640, 896), (896, 1152), (1152, 1280)]
 LAST_CHUNK = (0, 384)
 LAST_PIECES = [(0, 256), (256, 384)]
 CODES = 4
-SCALAR_EXPERTS = 5
+SCALAR_EXPERTS = 4
 SCALAR_WEIGHTS = [0, 1]
 WEIGHT_ORDER = [2, 0, 3, 1, 4, 5, 6, 7]
 

@@ -30,8 +30,9 @@ LAST_CHUNK = (0, 384)
 LAST_PIECES = [(0, 256), (256, 384)]
 CODES = 4
 SCALAR_EXPERTS = 4
-SCALAR_WEIGHTS = [0, 1]
-WEIGHT_ORDER = [2, 0, 3, 1, 4, 5, 6, 7]
+EARLY_WEIGHTS = [(12, 13), (13, 14)]
+LATE_WEIGHTS = [(e, e + 2) for e in range(0, 12, 2)]
+SCALAR_WEIGHTS = [(14, 16)]
 
 
 def tile_moe_shr_lin_none_kernel(tc, xT, w, gate, offs, pos1, pos2, pos3, out):
@@ -43,17 +44,25 @@ def tile_moe_shr_lin_none_kernel(tc, xT, w, gate, offs, pos1, pos2, pos3, out):
 
         x_rows = xT.rearrange("(p h j) t -> p h j t", h=2, j=2)
         x_raw = {}
-        offsets = keep.tile([P, SLOTS // STRIPE], U16, name="offsets")
-        for h in range(2):
-            for a, b in X_CHUNKS:
-                x_raw[h, a] = keep.tile([P, 2, b - a], F32, name="x_raw_%d_%d" % (h, a))
-                nc.sync.dma_start(x_raw[h, a][:], x_rows[:, h, :, a:b])
-            if h == 0:
-                nc.sync.dma_start(offsets[:], offs)
         w_raw = {}
-        for g in WEIGHT_ORDER:
-            w_raw[g] = keep.tile([P, 2, PACK, N], F32, name="w_raw_%d" % g)
-            nc.sync.dma_start(w_raw[g][:], w[2 * g : 2 * g + 2].rearrange("e (p j) n -> p e j n", j=PACK))
+        offsets = keep.tile([P, SLOTS // STRIPE], U16, name="offsets")
+
+        def load_x(h):
+            for a, b in X_CHUNKS:
+                x_raw[h, a] = keep.tile([P, 2, b - a], F32, name="x_raw_%d_%d" % (h, a), align_bytes=64)
+                nc.sync.dma_start(x_raw[h, a][:], x_rows[:, h, :, a:b])
+
+        def load_w(first, last):
+            w_raw[first] = keep.tile([P, last - first, PACK, N], F32, name="w_raw_%d" % first)
+            nc.sync.dma_start(w_raw[first][:], w[first:last].rearrange("e (p j) n -> p e j n", j=PACK))
+
+        load_x(0)
+        nc.sync.dma_start(offsets[:], offs)
+        for first, last in EARLY_WEIGHTS:
+            load_w(first, last)
+        load_x(1)
+        for first, last in LATE_WEIGHTS + SCALAR_WEIGHTS:
+            load_w(first, last)
         places = []
         gates = []
         for r, pos in enumerate((pos1, pos2, pos3)):
@@ -72,20 +81,16 @@ def tile_moe_shr_lin_none_kernel(tc, xT, w, gate, offs, pos1, pos2, pos3, out):
             nc.vector.tensor_copy(x_pairs[:, 0, a:b, :], x_raw[0, a][:].rearrange("p j t -> p t j"))
             for j in range(2):
                 nc.scalar.copy(x_planes[j][:, a:b], x_raw[0, a][:, j, :])
-        for a, b in X_CHUNKS:
-            nc.gpsimd.tensor_scalar(
-                x_pairs[:, 1, a:b, :], x_raw[1, a][:].rearrange("p j t -> p t j"), 1.0, 0.0, MULT, ADD
-            )
         x_words = x_pairs[:].rearrange("p h t j -> p (h t j)").bitcast(U32)
         x_halves = x_words.bitcast(F32).rearrange("p (h t) -> p t h", h=2)
 
         banks = [psum.tile([P, BANK], F32, name="bank_%d" % i) for i in range(BANKS)]
-        picked = [keep.tile([P, 2 * BANK], U32, name="picked_%d" % i, align_bytes=64) for i in range(count)]
-        grouped = [keep.tile([P, 2 * BANK], F32, name="grouped_%d" % i, align_bytes=64) for i in range(count)]
-        codes = [keep.tile([P, BANK], U32, name="codes_%d" % i, align_bytes=64) for i in range(CODES)]
+        picked = [keep.tile([P, 2 * BANK], U32, name="picked_%d" % i, tag="picked_%d" % i, align_bytes=64) for i in range(count)]
+        grouped = [keep.tile([P, 2 * BANK], F32, name="grouped_%d" % i, tag="grouped_%d" % i, align_bytes=64) for i in range(count)]
+        ring = [keep.tile([P, BANK], U32, name="codes_%d" % i, align_bytes=64) for i in range(CODES)]
+        codes = [ring[i % CODES] for i in range(count)]
         scales = [keep.tile([P, BANK], U8, name="scales_%d" % i, align_bytes=64) for i in range(CODES)]
         w_grouped = keep.tile([P, E + 1, N, PACK], BF16, name="w_grouped", align_bytes=64)
-        w_codes = keep.tile([P, (E + 1) * N], U32, name="w_codes", align_bytes=64)
         w_scales = keep.tile([P, (E + 1) * N], U8, name="w_scales", align_bytes=64)
         y = keep.tile([P, SLOTS], F32, name="y")
         ys = keep.tile([P, T], F32, name="ys")
@@ -113,29 +118,31 @@ def tile_moe_shr_lin_none_kernel(tc, xT, w, gate, offs, pos1, pos2, pos3, out):
                 picked[g][:].bitcast(F32).rearrange("p (h s) -> p s h", h=2)[:, : b - a, :],
             )
 
-        def round_weights(g):
-            if g in SCALAR_WEIGHTS:
-                for e in range(2):
-                    nc.scalar.copy(
-                        w_grouped[:, 2 * g + e].rearrange("p (c i) j -> p c j i", i=4),
-                        w_raw[g][:, e].rearrange("p j (c i) -> p c j i", i=4),
-                    )
-            else:
-                nc.gpsimd.tensor_scalar(
-                    w_grouped[:, 2 * g : 2 * g + 2], w_raw[g][:].rearrange("p e j n -> p e n j"), 1.0, 0.0, MULT, ADD
+        def round_weights_on_scalar(first, last):
+            for e in range(first, last):
+                nc.scalar.copy(
+                    w_grouped[:, e].rearrange("p (c i) j -> p c j i", i=4),
+                    w_raw[first][:, e - first].rearrange("p j (c i) -> p c j i", i=4),
                 )
+
+        def round_weights_on_gpsimd(first, last):
+            nc.gpsimd.tensor_scalar(
+                w_grouped[:, first:last], w_raw[first][:].rearrange("p e j n -> p e n j"), 1.0, 0.0, MULT, ADD
+            )
 
         def quantize_weights(g):
             cols = slice(2 * g * N, (2 * g + 2) * N)
+            tag = "grouped_%d" % (g - 2) if 2 * g == EARLY_WEIGHTS[0][0] else "w_codes_%d" % g
+            w_codes[g] = keep.tile([P, 2 * N], U32, name="w_codes_%d" % g, tag=tag, align_bytes=64)
             nc.vector.quantize_mx(
-                out=w_codes[:, cols].bitcast(FP8X4),
+                out=w_codes[g][:].bitcast(FP8X4),
                 scales=w_scales[:, cols],
                 in_=w_grouped[:, 2 * g : 2 * g + 2].rearrange("p e n j -> p (e n j)"),
             )
 
         def quantize_columns(i, source, width):
             nc.vector.quantize_mx(
-                out=codes[i % CODES][:, :width].bitcast(FP8X4),
+                out=codes[i][:, :width].bitcast(FP8X4),
                 scales=scales[i % CODES][:, :width],
                 in_=source[:, : 2 * width].bitcast(BF16),
             )
@@ -144,9 +151,9 @@ def tile_moe_shr_lin_none_kernel(tc, xT, w, gate, offs, pos1, pos2, pos3, out):
             w_cols = slice(e * N, (e + 1) * N)
             nc.tensor.matmul_mx(
                 out=acc,
-                lhsT=w_codes[:, w_cols].bitcast(FP8X4),
+                lhsT=w_codes[e // 2][:, e % 2 * N : (e % 2 + 1) * N].bitcast(FP8X4),
                 lhsT_scale=w_scales[:, w_cols],
-                rhs=codes[i % CODES][:, cols].bitcast(FP8X4),
+                rhs=codes[i][:, cols].bitcast(FP8X4),
                 rhs_scale=scales[i % CODES][:, cols],
                 start=True,
                 stop=True,
@@ -162,11 +169,8 @@ def tile_moe_shr_lin_none_kernel(tc, xT, w, gate, offs, pos1, pos2, pos3, out):
 
         def lay_tokens(s):
             a, b = SHARED[s]
-            rows = picked[(7 + s) % count][:, : 2 * (b - a)].bitcast(F32)
-            if s < 1:
-                nc.vector.tensor_copy(rows.rearrange("p (t h) -> p t h", h=2), x_halves[:, a:b, :])
-            else:
-                nc.scalar.copy(rows.rearrange("p (t h) -> p t h", h=2), x_halves[:, a:b, :])
+            rows = x_raw[0, a][:].rearrange("p j t -> p (j t)")
+            nc.scalar.copy(rows.rearrange("p (t h) -> p t h", h=2), x_halves[:, a:b, :])
             return rows
 
         def shared_expert(s, rows):
@@ -182,6 +186,14 @@ def tile_moe_shr_lin_none_kernel(tc, xT, w, gate, offs, pos1, pos2, pos3, out):
             )
             return term[:]
 
+        for first, last in EARLY_WEIGHTS:
+            round_weights_on_gpsimd(first, last)
+        for a, b in X_CHUNKS:
+            nc.gpsimd.tensor_scalar(
+                x_pairs[:, 1, a:b, :], x_raw[1, a][:].rearrange("p j t -> p t j"), 1.0, 0.0, MULT, ADD
+            )
+        for first, last in LATE_WEIGHTS:
+            round_weights_on_gpsimd(first, last)
         for j in range(2):
             for e in range(SCALAR_EXPERTS):
                 gather_values(e, j)
@@ -190,14 +202,17 @@ def tile_moe_shr_lin_none_kernel(tc, xT, w, gate, offs, pos1, pos2, pos3, out):
                 gather_words(0, g, max(a, SCALAR_EXPERTS * C))
         for g, (a, b) in enumerate(GROUPS):
             gather_words(1, g, a)
-        for g in WEIGHT_ORDER:
-            round_weights(g)
+        rows = [lay_tokens(s) for s in range(len(SHARED))]
+        for first, last in SCALAR_WEIGHTS:
+            round_weights_on_scalar(first, last)
         for g in range(count):
             interleave(g)
-        rows = [lay_tokens(s) for s in range(len(SHARED))]
+        w_codes = {}
         for g in range(count):
             quantize_weights(g)
             experts(g)
+        shared_codes = keep.tile([P, T], U32, name="shared_codes", tag="picked_%d" % (count - 1), align_bytes=64)
+        codes.extend(shared_codes[:, a:b] for a, b in SHARED)
         for s in range(len(SHARED)):
             shared_expert(s, rows[s])
 

@@ -29,10 +29,10 @@ OUT_CHUNKS = [(384, 640), (640, 896), (896, 1152), (1152, 1280)]
 LAST_CHUNK = (0, 384)
 LAST_PIECES = [(0, 256), (256, 384)]
 CODES = 4
-SCALAR_EXPERTS = 4
-EARLY_WEIGHTS = [(12, 13), (13, 14)]
+SCALAR_SLOTS = [512, 256, 160]
+EARLY_WEIGHTS = [(12, 13)]
 LATE_WEIGHTS = [(e, e + 2) for e in range(0, 12, 2)]
-SCALAR_WEIGHTS = [(14, 16)]
+SCALAR_WEIGHTS = [(13, 14), (14, 16)]
 
 
 def tile_moe_shr_lin_none_kernel(tc, xT, w, gate, offs, pos1, pos2, pos3, out):
@@ -47,8 +47,8 @@ def tile_moe_shr_lin_none_kernel(tc, xT, w, gate, offs, pos1, pos2, pos3, out):
         w_raw = {}
         offsets = keep.tile([P, SLOTS // STRIPE], U16, name="offsets")
 
-        def load_x(h):
-            for a, b in X_CHUNKS:
+        def load_x(h, chunks):
+            for a, b in chunks:
                 x_raw[h, a] = keep.tile([P, 2, b - a], F32, name="x_raw_%d_%d" % (h, a), align_bytes=64)
                 nc.sync.dma_start(x_raw[h, a][:], x_rows[:, h, :, a:b])
 
@@ -56,11 +56,11 @@ def tile_moe_shr_lin_none_kernel(tc, xT, w, gate, offs, pos1, pos2, pos3, out):
             w_raw[first] = keep.tile([P, last - first, PACK, N], F32, name="w_raw_%d" % first)
             nc.sync.dma_start(w_raw[first][:], w[first:last].rearrange("e (p j) n -> p e j n", j=PACK))
 
-        load_x(0)
+        load_x(0, X_CHUNKS)
         nc.sync.dma_start(offsets[:], offs)
         for first, last in EARLY_WEIGHTS:
             load_w(first, last)
-        load_x(1)
+        load_x(1, X_CHUNKS[::-1])
         for first, last in LATE_WEIGHTS + SCALAR_WEIGHTS:
             load_w(first, last)
         places = []
@@ -102,13 +102,12 @@ def tile_moe_shr_lin_none_kernel(tc, xT, w, gate, offs, pos1, pos2, pos3, out):
                 x_words[:, h * T : (h + 1) * T].indirect(offsets[:, start // STRIPE : b // STRIPE]),
             )
 
-        def gather_values(e, j):
-            g, first = divmod(e * C, BANK)
+        def gather_values(g, j):
+            a = GROUPS[g][0]
+            b = a + SCALAR_SLOTS[g]
             pairs = picked[g][:, :BANK].bitcast(BF16).rearrange("p (s j) -> p s j", j=2)
             nc.scalar.activation(
-                pairs[:, first : first + C, j],
-                x_planes[j][:].indirect(offsets[:, e * C // STRIPE : (e + 1) * C // STRIPE]),
-                COPY,
+                pairs[:, : b - a, j], x_planes[j][:].indirect(offsets[:, a // STRIPE : b // STRIPE]), COPY
             )
 
         def interleave(g):
@@ -132,8 +131,7 @@ def tile_moe_shr_lin_none_kernel(tc, xT, w, gate, offs, pos1, pos2, pos3, out):
 
         def quantize_weights(g):
             cols = slice(2 * g * N, (2 * g + 2) * N)
-            tag = "grouped_%d" % (g - 2) if 2 * g == EARLY_WEIGHTS[0][0] else "w_codes_%d" % g
-            w_codes[g] = keep.tile([P, 2 * N], U32, name="w_codes_%d" % g, tag=tag, align_bytes=64)
+            w_codes[g] = keep.tile([P, 2 * N], U32, name="w_codes_%d" % g, align_bytes=64)
             nc.vector.quantize_mx(
                 out=w_codes[g][:].bitcast(FP8X4),
                 scales=w_scales[:, cols],
@@ -188,18 +186,19 @@ def tile_moe_shr_lin_none_kernel(tc, xT, w, gate, offs, pos1, pos2, pos3, out):
 
         for first, last in EARLY_WEIGHTS:
             round_weights_on_gpsimd(first, last)
-        for a, b in X_CHUNKS:
+        for a, b in X_CHUNKS[::-1]:
             nc.gpsimd.tensor_scalar(
                 x_pairs[:, 1, a:b, :], x_raw[1, a][:].rearrange("p j t -> p t j"), 1.0, 0.0, MULT, ADD
             )
         for first, last in LATE_WEIGHTS:
             round_weights_on_gpsimd(first, last)
         for j in range(2):
-            for e in range(SCALAR_EXPERTS):
-                gather_values(e, j)
+            for g in range(len(SCALAR_SLOTS)):
+                gather_values(g, j)
         for g, (a, b) in enumerate(GROUPS):
-            if b > SCALAR_EXPERTS * C:
-                gather_words(0, g, max(a, SCALAR_EXPERTS * C))
+            start = a + (SCALAR_SLOTS[g] if g < len(SCALAR_SLOTS) else 0)
+            if start < b:
+                gather_words(0, g, start)
         for g, (a, b) in enumerate(GROUPS):
             gather_words(1, g, a)
         rows = [lay_tokens(s) for s in range(len(SHARED))]

@@ -29,10 +29,11 @@ OUT_CHUNKS = [(384, 640), (640, 896), (896, 1152), (1152, 1280)]
 LAST_CHUNK = (0, 384)
 LAST_PIECES = [(0, 256), (256, 384)]
 CODES = 4
-SCALAR_SLOTS = [512, 256, 160]
+SCALAR_SLOTS = [512, 256, 224]
+SPLIT = 13
 EARLY_WEIGHTS = [(12, 13)]
 LATE_WEIGHTS = [(e, e + 2) for e in range(0, 12, 2)]
-SCALAR_WEIGHTS = [(13, 14), (14, 16)]
+SCALAR_WEIGHTS = [(14, 16)]
 
 
 def tile_moe_shr_lin_none_kernel(tc, xT, w, gate, offs, pos1, pos2, pos3, out):
@@ -61,7 +62,7 @@ def tile_moe_shr_lin_none_kernel(tc, xT, w, gate, offs, pos1, pos2, pos3, out):
         for first, last in EARLY_WEIGHTS:
             load_w(first, last)
         load_x(1, X_CHUNKS[::-1])
-        for first, last in LATE_WEIGHTS + SCALAR_WEIGHTS:
+        for first, last in LATE_WEIGHTS + [(SPLIT, SPLIT + 1)] + SCALAR_WEIGHTS:
             load_w(first, last)
         places = []
         gates = []
@@ -129,13 +130,15 @@ def tile_moe_shr_lin_none_kernel(tc, xT, w, gate, offs, pos1, pos2, pos3, out):
                 w_grouped[:, first:last], w_raw[first][:].rearrange("p e j n -> p e n j"), 1.0, 0.0, MULT, ADD
             )
 
-        def quantize_weights(g):
-            cols = slice(2 * g * N, (2 * g + 2) * N)
-            w_codes[g] = keep.tile([P, 2 * N], U32, name="w_codes_%d" % g, align_bytes=64)
+        def quantize_weights(first, last, tag):
+            cols = slice(first * N, last * N)
+            made = keep.tile([P, (last - first) * N], U32, name="w_codes_%d" % first, tag=tag, align_bytes=64)
+            for e in range(first, last):
+                w_codes[e] = made[:, (e - first) * N : (e - first + 1) * N]
             nc.vector.quantize_mx(
-                out=w_codes[g][:].bitcast(FP8X4),
+                out=made[:].bitcast(FP8X4),
                 scales=w_scales[:, cols],
-                in_=w_grouped[:, 2 * g : 2 * g + 2].rearrange("p e n j -> p (e n j)"),
+                in_=w_grouped[:, first:last].rearrange("p e n j -> p (e n j)"),
             )
 
         def quantize_columns(i, source, width):
@@ -149,7 +152,7 @@ def tile_moe_shr_lin_none_kernel(tc, xT, w, gate, offs, pos1, pos2, pos3, out):
             w_cols = slice(e * N, (e + 1) * N)
             nc.tensor.matmul_mx(
                 out=acc,
-                lhsT=w_codes[e // 2][:, e % 2 * N : (e % 2 + 1) * N].bitcast(FP8X4),
+                lhsT=w_codes[e].bitcast(FP8X4),
                 lhsT_scale=w_scales[:, w_cols],
                 rhs=codes[i][:, cols].bitcast(FP8X4),
                 rhs_scale=scales[i % CODES][:, cols],
@@ -192,6 +195,14 @@ def tile_moe_shr_lin_none_kernel(tc, xT, w, gate, offs, pos1, pos2, pos3, out):
             )
         for first, last in LATE_WEIGHTS:
             round_weights_on_gpsimd(first, last)
+        nc.gpsimd.tensor_scalar(
+            w_grouped[:, SPLIT, : N // 2],
+            w_raw[SPLIT][:, 0, :, : N // 2].rearrange("p j n -> p n j"),
+            1.0,
+            0.0,
+            MULT,
+            ADD,
+        )
         for j in range(2):
             for g in range(len(SCALAR_SLOTS)):
                 gather_values(g, j)
@@ -202,16 +213,26 @@ def tile_moe_shr_lin_none_kernel(tc, xT, w, gate, offs, pos1, pos2, pos3, out):
         for g, (a, b) in enumerate(GROUPS):
             gather_words(1, g, a)
         rows = [lay_tokens(s) for s in range(len(SHARED))]
+        nc.scalar.copy(
+            w_grouped[:, SPLIT, N // 2 :].rearrange("p (c i) j -> p c j i", i=4),
+            w_raw[SPLIT][:, 0, :, N // 2 :].rearrange("p j (c i) -> p c j i", i=4),
+        )
         for first, last in SCALAR_WEIGHTS:
             round_weights_on_scalar(first, last)
         for g in range(count):
             interleave(g)
         w_codes = {}
         for g in range(count):
-            quantize_weights(g)
+            quantize_weights(2 * g, min(2 * g + 2, E), "w_codes_%d" % g)
             experts(g)
-        shared_codes = keep.tile([P, T], U32, name="shared_codes", tag="picked_%d" % (count - 1), align_bytes=64)
+        shared_codes = keep.tile([P, T + N], U32, name="shared_codes", tag="picked_%d" % (count - 1), align_bytes=64)
         codes.extend(shared_codes[:, a:b] for a, b in SHARED)
+        w_codes[E] = shared_codes[:, T:]
+        nc.vector.quantize_mx(
+            out=w_codes[E].bitcast(FP8X4),
+            scales=w_scales[:, E * N :],
+            in_=w_grouped[:, E].rearrange("p n j -> p (n j)"),
+        )
         for s in range(len(SHARED)):
             shared_expert(s, rows[s])
 

@@ -29,7 +29,10 @@ OUT_CHUNKS = [(384, 640), (640, 896), (896, 1152), (1152, 1280)]
 LAST_CHUNK = (0, 384)
 LAST_PIECES = [(0, 256), (256, 384)]
 CODES = 4
-SCALAR_SLOTS = [512, 256, 224]
+SPAN = 2 * BANK
+SPANS = [(s, min(s + SPAN, SLOTS)) for s in range(0, SLOTS, SPAN)]
+WINDOW = T + 96
+EARLY, LATE = 1, 0
 SPLIT = 13
 EARLY_WEIGHTS = [(12, 13)]
 LATE_WEIGHTS = [(e, e + 2) for e in range(0, 12, 2)]
@@ -57,11 +60,11 @@ def tile_moe_shr_lin_none_kernel(tc, xT, w, gate, offs, pos1, pos2, pos3, out):
             w_raw[first] = keep.tile([P, last - first, PACK, N], F32, name="w_raw_%d" % first)
             nc.sync.dma_start(w_raw[first][:], w[first:last].rearrange("e (p j) n -> p e j n", j=PACK))
 
-        load_x(0, X_CHUNKS)
+        load_x(EARLY, X_CHUNKS)
         nc.sync.dma_start(offsets[:], offs)
         for first, last in EARLY_WEIGHTS:
             load_w(first, last)
-        load_x(1, X_CHUNKS[::-1])
+        load_x(LATE, X_CHUNKS[::-1])
         for first, last in LATE_WEIGHTS + [(SPLIT, SPLIT + 1)] + SCALAR_WEIGHTS:
             load_w(first, last)
         places = []
@@ -76,46 +79,52 @@ def tile_moe_shr_lin_none_kernel(tc, xT, w, gate, offs, pos1, pos2, pos3, out):
         identity = keep.tile([P, P], F32, name="identity")
         make_identity(nc, identity[:])
 
-        x_pairs = keep.tile([P, 2, T, 2], BF16, name="x_pairs", align_bytes=64)
+        x_both = keep.tile([P, 2 * (T + WINDOW)], BF16, name="x_both", align_bytes=64)
+        nc.vector.memset(x_both[:, 4 * T :], 0.0)
+        x_pairs = [x_both[:, 2 * T * h : 2 * T * (h + 1)].rearrange("p (t j) -> p t j", j=2) for h in range(2)]
         x_planes = [keep.tile([P, T], BF16, name="x_plane_%d" % j) for j in range(2)]
         for a, b in X_CHUNKS:
-            nc.vector.tensor_copy(x_pairs[:, 0, a:b, :], x_raw[0, a][:].rearrange("p j t -> p t j"))
+            nc.vector.tensor_copy(x_pairs[EARLY][:, a:b, :], x_raw[EARLY, a][:].rearrange("p j t -> p t j"))
             for j in range(2):
-                nc.scalar.copy(x_planes[j][:, a:b], x_raw[0, a][:, j, :])
-        x_words = x_pairs[:].rearrange("p h t j -> p (h t j)").bitcast(U32)
-        x_halves = x_words.bitcast(F32).rearrange("p (h t) -> p t h", h=2)
+                nc.scalar.copy(x_planes[j][:, a:b], x_raw[EARLY, a][:, j, :])
+        x_words = x_both[:].bitcast(U32)
+        x_halves = x_words[:, : 2 * T].bitcast(F32).rearrange("p (h t) -> p t h", h=2)
 
         banks = [psum.tile([P, BANK], F32, name="bank_%d" % i) for i in range(BANKS)]
-        picked = [keep.tile([P, 2 * BANK], U32, name="picked_%d" % i, tag="picked_%d" % i, align_bytes=64) for i in range(count)]
+        picked = [
+            keep.tile([P, 2 * SPAN], U32, name="picked_%d" % i, tag="picked_%d" % i, align_bytes=64)
+            for i in range(len(SPANS))
+        ]
         grouped = [keep.tile([P, 2 * BANK], F32, name="grouped_%d" % i, tag="grouped_%d" % i, align_bytes=64) for i in range(count)]
         ring = [keep.tile([P, BANK], U32, name="codes_%d" % i, align_bytes=64) for i in range(CODES)]
         codes = [ring[i % CODES] for i in range(count)]
         scales = [keep.tile([P, BANK], U8, name="scales_%d" % i, align_bytes=64) for i in range(CODES)]
         w_grouped = keep.tile([P, E + 1, N, PACK], BF16, name="w_grouped", align_bytes=64)
         w_scales = keep.tile([P, (E + 1) * N], U8, name="w_scales", align_bytes=64)
+        singles = keep.tile([P, 2 * SPAN], BF16, name="singles")
         y = keep.tile([P, SLOTS], F32, name="y")
         ys = keep.tile([P, T], F32, name="ys")
 
-        def gather_words(h, g, start):
-            a, b = GROUPS[g]
+        def gather_words(h, u):
+            a, b = SPANS[u]
             nc.vector.tensor_copy(
-                picked[g][:, h * BANK + start - a : h * BANK + b - a],
-                x_words[:, h * T : (h + 1) * T].indirect(offsets[:, start // STRIPE : b // STRIPE]),
+                picked[u][:, h * SPAN : h * SPAN + b - a],
+                x_words[:, h * T : h * T + WINDOW].indirect(offsets[:, a // STRIPE : b // STRIPE]),
             )
 
         def gather_values(g, j):
-            a = GROUPS[g][0]
-            b = a + SCALAR_SLOTS[g]
-            pairs = picked[g][:, :BANK].bitcast(BF16).rearrange("p (s j) -> p s j", j=2)
+            a, b = GROUPS[g]
             nc.scalar.activation(
-                pairs[:, : b - a, j], x_planes[j][:].indirect(offsets[:, a // STRIPE : b // STRIPE]), COPY
+                singles[:, j * SPAN + a : j * SPAN + b],
+                x_planes[j][:].indirect(offsets[:, a // STRIPE : b // STRIPE]),
+                COPY,
             )
 
         def interleave(g):
             a, b = GROUPS[g]
             nc.scalar.copy(
                 grouped[g][:, : 2 * (b - a)].rearrange("p (s h) -> p s h", h=2),
-                picked[g][:].bitcast(F32).rearrange("p (h s) -> p s h", h=2)[:, : b - a, :],
+                picked[a // SPAN][:].bitcast(F32).rearrange("p (h s) -> p s h", h=2)[:, a % SPAN : a % SPAN + b - a, :],
             )
 
         def round_weights_on_scalar(first, last):
@@ -170,7 +179,7 @@ def tile_moe_shr_lin_none_kernel(tc, xT, w, gate, offs, pos1, pos2, pos3, out):
 
         def lay_tokens(s):
             a, b = SHARED[s]
-            rows = x_raw[0, a][:].rearrange("p j t -> p (j t)")
+            rows = x_raw[EARLY, a][:].rearrange("p j t -> p (j t)")
             nc.scalar.copy(rows.rearrange("p (t h) -> p t h", h=2), x_halves[:, a:b, :])
             return rows
 
@@ -191,7 +200,7 @@ def tile_moe_shr_lin_none_kernel(tc, xT, w, gate, offs, pos1, pos2, pos3, out):
             round_weights_on_gpsimd(first, last)
         for a, b in X_CHUNKS[::-1]:
             nc.gpsimd.tensor_scalar(
-                x_pairs[:, 1, a:b, :], x_raw[1, a][:].rearrange("p j t -> p t j"), 1.0, 0.0, MULT, ADD
+                x_pairs[LATE][:, a:b, :], x_raw[LATE, a][:].rearrange("p j t -> p t j"), 1.0, 0.0, MULT, ADD
             )
         for first, last in LATE_WEIGHTS:
             round_weights_on_gpsimd(first, last)
@@ -204,14 +213,16 @@ def tile_moe_shr_lin_none_kernel(tc, xT, w, gate, offs, pos1, pos2, pos3, out):
             ADD,
         )
         for j in range(2):
-            for g in range(len(SCALAR_SLOTS)):
+            for g in range(SPAN // BANK):
                 gather_values(g, j)
-        for g, (a, b) in enumerate(GROUPS):
-            start = a + (SCALAR_SLOTS[g] if g < len(SCALAR_SLOTS) else 0)
-            if start < b:
-                gather_words(0, g, start)
-        for g, (a, b) in enumerate(GROUPS):
-            gather_words(1, g, a)
+        nc.scalar.copy(
+            picked[0][:, EARLY * SPAN : (EARLY + 1) * SPAN].bitcast(BF16).rearrange("p (s j) -> p s j", j=2),
+            singles[:].rearrange("p (j s) -> p s j", j=2),
+        )
+        for u in range(1, len(SPANS)):
+            gather_words(EARLY, u)
+        for u in range(len(SPANS)):
+            gather_words(LATE, u)
         rows = [lay_tokens(s) for s in range(len(SHARED))]
         nc.scalar.copy(
             w_grouped[:, SPLIT, N // 2 :].rearrange("p (c i) j -> p c j i", i=4),
@@ -225,7 +236,7 @@ def tile_moe_shr_lin_none_kernel(tc, xT, w, gate, offs, pos1, pos2, pos3, out):
         for g in range(count):
             quantize_weights(2 * g, min(2 * g + 2, E), "w_codes_%d" % g)
             experts(g)
-        shared_codes = keep.tile([P, T + N], U32, name="shared_codes", tag="picked_%d" % (count - 1), align_bytes=64)
+        shared_codes = keep.tile([P, T + N], U32, name="shared_codes", tag="picked_%d" % (len(SPANS) - 1), align_bytes=64)
         codes.extend(shared_codes[:, a:b] for a, b in SHARED)
         w_codes[E] = shared_codes[:, T:]
         nc.vector.quantize_mx(

@@ -22,21 +22,29 @@ PACK = 4
 STRIPE = 16
 BANK = 512
 BANKS = 8
-X_CHUNKS = [(0, 512), (512, 1024), (1024, 1280)]
+EARLY, LATE = 1, 0
+
+EARLY_CHUNKS = [(0, 512), (512, 768), (768, 1024), (1024, 1152), (1152, 1280)]
+LATE_CHUNKS = [(1024, 1280), (512, 1024), (0, 512)]
+
 GROUPS = [(s, min(s + BANK, SLOTS)) for s in range(0, SLOTS, BANK)]
 SHARED = [(s, min(s + BANK, T)) for s in range(0, T, BANK)]
-OUT_CHUNKS = [(384, 640), (640, 896), (896, 1152), (1152, 1280)]
-LAST_CHUNK = (0, 384)
-LAST_PIECES = [(0, 256), (256, 384)]
-CODES = 4
-SPAN = 2 * BANK
-SPANS = [(s, min(s + SPAN, SLOTS)) for s in range(0, SLOTS, SPAN)]
-WINDOW = T + 96
-EARLY, LATE = 1, 0
-SPLIT = 13
-EARLY_WEIGHTS = [(12, 13)]
-LATE_WEIGHTS = [(e, e + 2) for e in range(0, 12, 2)]
-SCALAR_WEIGHTS = [(14, 16)]
+CODE_TILES = 4
+
+SCALAR_SLOTS = 960
+SPAN = 4 * BANK
+SECOND_MIDDLE = (SPAN + SLOTS) // 2
+EARLY_RUNS = [(SCALAR_SLOTS, SPAN), (SPAN, SECOND_MIDDLE), (SECOND_MIDDLE, SLOTS)]
+LATE_RUNS = [(0, SPAN // 2), (SPAN // 2, SPAN), (SPAN, SECOND_MIDDLE), (SECOND_MIDDLE, SLOTS)]
+WINDOW = T + 176
+
+PRELOADED_WEIGHTS = (12, 13)
+GPSIMD_WEIGHTS = [(e, e + 2) for e in range(0, 12, 2)]
+SCALAR_WEIGHTS = [(13, 14), (14, 16)]
+
+VECTOR_TOKENS = 384
+VECTOR_PIECES = [(0, 256), (256, VECTOR_TOKENS)]
+TENSOR_CHUNKS = [(VECTOR_TOKENS, 640), (640, 896), (896, 1152), (1152, T)]
 
 
 def tile_moe_shr_lin_none_kernel(tc, xT, w, gate, offs, pos1, pos2, pos3, out):
@@ -60,12 +68,11 @@ def tile_moe_shr_lin_none_kernel(tc, xT, w, gate, offs, pos1, pos2, pos3, out):
             w_raw[first] = keep.tile([P, last - first, PACK, N], F32, name="w_raw_%d" % first)
             nc.sync.dma_start(w_raw[first][:], w[first:last].rearrange("e (p j) n -> p e j n", j=PACK))
 
-        load_x(EARLY, X_CHUNKS)
+        load_x(EARLY, EARLY_CHUNKS)
         nc.sync.dma_start(offsets[:], offs)
-        for first, last in EARLY_WEIGHTS:
-            load_w(first, last)
-        load_x(LATE, X_CHUNKS[::-1])
-        for first, last in LATE_WEIGHTS + [(SPLIT, SPLIT + 1)] + SCALAR_WEIGHTS:
+        load_w(*PRELOADED_WEIGHTS)
+        load_x(LATE, LATE_CHUNKS)
+        for first, last in GPSIMD_WEIGHTS + SCALAR_WEIGHTS:
             load_w(first, last)
         places = []
         gates = []
@@ -83,7 +90,7 @@ def tile_moe_shr_lin_none_kernel(tc, xT, w, gate, offs, pos1, pos2, pos3, out):
         nc.vector.memset(x_both[:, 4 * T :], 0.0)
         x_pairs = [x_both[:, 2 * T * h : 2 * T * (h + 1)].rearrange("p (t j) -> p t j", j=2) for h in range(2)]
         x_planes = [keep.tile([P, T], BF16, name="x_plane_%d" % j) for j in range(2)]
-        for a, b in X_CHUNKS:
+        for a, b in EARLY_CHUNKS:
             nc.vector.tensor_copy(x_pairs[EARLY][:, a:b, :], x_raw[EARLY, a][:].rearrange("p j t -> p t j"))
             for j in range(2):
                 nc.scalar.copy(x_planes[j][:, a:b], x_raw[EARLY, a][:, j, :])
@@ -92,39 +99,39 @@ def tile_moe_shr_lin_none_kernel(tc, xT, w, gate, offs, pos1, pos2, pos3, out):
 
         banks = [psum.tile([P, BANK], F32, name="bank_%d" % i) for i in range(BANKS)]
         picked = [
-            keep.tile([P, 2 * SPAN], U32, name="picked_%d" % i, tag="picked_%d" % i, align_bytes=64)
-            for i in range(len(SPANS))
+            keep.tile([P, 2 * SPAN], U32, name="picked_%d" % i, tag="picked_%d" % i, align_bytes=64) for i in range(2)
         ]
-        grouped = [keep.tile([P, 2 * BANK], F32, name="grouped_%d" % i, tag="grouped_%d" % i, align_bytes=64) for i in range(count)]
-        ring = [keep.tile([P, BANK], U32, name="codes_%d" % i, align_bytes=64) for i in range(CODES)]
-        codes = [ring[i % CODES] for i in range(count)]
-        scales = [keep.tile([P, BANK], U8, name="scales_%d" % i, align_bytes=64) for i in range(CODES)]
+        grouped = [keep.tile([P, 2 * BANK], F32, name="grouped_%d" % i, align_bytes=64) for i in range(count)]
+        ring = [keep.tile([P, BANK], U32, name="codes_%d" % i, align_bytes=64) for i in range(CODE_TILES)]
+        codes = [ring[i % CODE_TILES] for i in range(count)]
+        scales = [keep.tile([P, BANK], U8, name="scales_%d" % i, align_bytes=64) for i in range(CODE_TILES)]
         w_grouped = keep.tile([P, E + 1, N, PACK], BF16, name="w_grouped", align_bytes=64)
         w_scales = keep.tile([P, (E + 1) * N], U8, name="w_scales", align_bytes=64)
-        singles = keep.tile([P, 2 * SPAN], BF16, name="singles")
+        w_codes = {}
+        singles = keep.tile([P, 2 * SCALAR_SLOTS], BF16, name="singles")
         y = keep.tile([P, SLOTS], F32, name="y")
         ys = keep.tile([P, T], F32, name="ys")
 
-        def gather_words(h, u):
-            a, b = SPANS[u]
+        def gather_pairs(h, a, b):
+            start = h * SPAN + a % SPAN
             nc.vector.tensor_copy(
-                picked[u][:, h * SPAN : h * SPAN + b - a],
+                picked[a // SPAN][:, start : start + b - a],
                 x_words[:, h * T : h * T + WINDOW].indirect(offsets[:, a // STRIPE : b // STRIPE]),
             )
 
-        def gather_values(g, j):
-            a, b = GROUPS[g]
+        def gather_values(j, a, b):
             nc.scalar.activation(
-                singles[:, j * SPAN + a : j * SPAN + b],
+                singles[:, j * SCALAR_SLOTS + a : j * SCALAR_SLOTS + b],
                 x_planes[j][:].indirect(offsets[:, a // STRIPE : b // STRIPE]),
                 COPY,
             )
 
         def interleave(g):
             a, b = GROUPS[g]
+            halves = picked[a // SPAN][:].bitcast(F32).rearrange("p (h s) -> p s h", h=2)
             nc.scalar.copy(
                 grouped[g][:, : 2 * (b - a)].rearrange("p (s h) -> p s h", h=2),
-                picked[a // SPAN][:].bitcast(F32).rearrange("p (h s) -> p s h", h=2)[:, a % SPAN : a % SPAN + b - a, :],
+                halves[:, a % SPAN : a % SPAN + b - a, :],
             )
 
         def round_weights_on_scalar(first, last):
@@ -134,37 +141,35 @@ def tile_moe_shr_lin_none_kernel(tc, xT, w, gate, offs, pos1, pos2, pos3, out):
                     w_raw[first][:, e - first].rearrange("p j (c i) -> p c j i", i=4),
                 )
 
-        def round_weights_on_gpsimd(first, last):
-            nc.gpsimd.tensor_scalar(
-                w_grouped[:, first:last], w_raw[first][:].rearrange("p e j n -> p e n j"), 1.0, 0.0, MULT, ADD
-            )
+        def round_on_gpsimd(rounded, raw):
+            nc.gpsimd.tensor_scalar(rounded, raw, 1.0, 0.0, MULT, ADD)
 
-        def quantize_weights(first, last, tag):
-            cols = slice(first * N, last * N)
-            made = keep.tile([P, (last - first) * N], U32, name="w_codes_%d" % first, tag=tag, align_bytes=64)
+        def round_weights_on_gpsimd(first, last):
+            round_on_gpsimd(w_grouped[:, first:last], w_raw[first][:].rearrange("p e j n -> p e n j"))
+
+        def quantize_weights(first, last, made):
             for e in range(first, last):
                 w_codes[e] = made[:, (e - first) * N : (e - first + 1) * N]
             nc.vector.quantize_mx(
-                out=made[:].bitcast(FP8X4),
-                scales=w_scales[:, cols],
+                out=made.bitcast(FP8X4),
+                scales=w_scales[:, first * N : last * N],
                 in_=w_grouped[:, first:last].rearrange("p e n j -> p (e n j)"),
             )
 
         def quantize_columns(i, source, width):
             nc.vector.quantize_mx(
                 out=codes[i][:, :width].bitcast(FP8X4),
-                scales=scales[i % CODES][:, :width],
+                scales=scales[i % CODE_TILES][:, :width],
                 in_=source[:, : 2 * width].bitcast(BF16),
             )
 
         def multiply(acc, e, i, cols):
-            w_cols = slice(e * N, (e + 1) * N)
             nc.tensor.matmul_mx(
                 out=acc,
                 lhsT=w_codes[e].bitcast(FP8X4),
-                lhsT_scale=w_scales[:, w_cols],
+                lhsT_scale=w_scales[:, e * N : (e + 1) * N],
                 rhs=codes[i][:, cols].bitcast(FP8X4),
-                rhs_scale=scales[i % CODES][:, cols],
+                rhs_scale=scales[i % CODE_TILES][:, cols],
                 start=True,
                 stop=True,
             )
@@ -179,7 +184,7 @@ def tile_moe_shr_lin_none_kernel(tc, xT, w, gate, offs, pos1, pos2, pos3, out):
 
         def lay_tokens(s):
             a, b = SHARED[s]
-            rows = x_raw[EARLY, a][:].rearrange("p j t -> p (j t)")
+            rows = x_raw[LATE, a][:].rearrange("p j t -> p (j t)")
             nc.scalar.copy(rows.rearrange("p (t h) -> p t h", h=2), x_halves[:, a:b, :])
             return rows
 
@@ -196,64 +201,47 @@ def tile_moe_shr_lin_none_kernel(tc, xT, w, gate, offs, pos1, pos2, pos3, out):
             )
             return term[:]
 
-        for first, last in EARLY_WEIGHTS:
+        round_weights_on_gpsimd(*PRELOADED_WEIGHTS)
+        for a, b in LATE_CHUNKS:
+            round_on_gpsimd(x_pairs[LATE][:, a:b, :], x_raw[LATE, a][:].rearrange("p j t -> p t j"))
+        for first, last in GPSIMD_WEIGHTS:
             round_weights_on_gpsimd(first, last)
-        for a, b in X_CHUNKS[::-1]:
-            nc.gpsimd.tensor_scalar(
-                x_pairs[LATE][:, a:b, :], x_raw[LATE, a][:].rearrange("p j t -> p t j"), 1.0, 0.0, MULT, ADD
-            )
-        for first, last in LATE_WEIGHTS:
-            round_weights_on_gpsimd(first, last)
-        nc.gpsimd.tensor_scalar(
-            w_grouped[:, SPLIT, : N // 2],
-            w_raw[SPLIT][:, 0, :, : N // 2].rearrange("p j n -> p n j"),
-            1.0,
-            0.0,
-            MULT,
-            ADD,
-        )
         for j in range(2):
-            for g in range(SPAN // BANK):
-                gather_values(g, j)
+            gather_values(j, 0, BANK)
+            gather_values(j, BANK, SCALAR_SLOTS)
         nc.scalar.copy(
-            picked[0][:, EARLY * SPAN : (EARLY + 1) * SPAN].bitcast(BF16).rearrange("p (s j) -> p s j", j=2),
+            picked[0][:, EARLY * SPAN : EARLY * SPAN + SCALAR_SLOTS].bitcast(BF16).rearrange("p (s j) -> p s j", j=2),
             singles[:].rearrange("p (j s) -> p s j", j=2),
         )
-        for u in range(1, len(SPANS)):
-            gather_words(EARLY, u)
-        for u in range(len(SPANS)):
-            gather_words(LATE, u)
-        rows = [lay_tokens(s) for s in range(len(SHARED))]
-        nc.scalar.copy(
-            w_grouped[:, SPLIT, N // 2 :].rearrange("p (c i) j -> p c j i", i=4),
-            w_raw[SPLIT][:, 0, :, N // 2 :].rearrange("p j (c i) -> p c j i", i=4),
-        )
+        for a, b in EARLY_RUNS:
+            gather_pairs(EARLY, a, b)
+        for a, b in LATE_RUNS:
+            gather_pairs(LATE, a, b)
+        laid = [lay_tokens(s) for s in range(len(SHARED))]
         for first, last in SCALAR_WEIGHTS:
             round_weights_on_scalar(first, last)
         for g in range(count):
             interleave(g)
-        w_codes = {}
-        for g in range(count):
-            quantize_weights(2 * g, min(2 * g + 2, E), "w_codes_%d" % g)
+
+        for g, (a, b) in enumerate(GROUPS):
+            made = keep.tile([P, (b - a) // C * N], U32, name="w_codes_%d" % g, align_bytes=64)
+            quantize_weights(a // C, b // C, made[:])
             experts(g)
-        shared_codes = keep.tile([P, T + N], U32, name="shared_codes", tag="picked_%d" % (len(SPANS) - 1), align_bytes=64)
+
+        shared_codes = keep.tile([P, T + N], U32, name="shared_codes", tag="picked_1", align_bytes=64)
         codes.extend(shared_codes[:, a:b] for a, b in SHARED)
-        w_codes[E] = shared_codes[:, T:]
-        nc.vector.quantize_mx(
-            out=w_codes[E].bitcast(FP8X4),
-            scales=w_scales[:, E * N :],
-            in_=w_grouped[:, E].rearrange("p n j -> p (n j)"),
-        )
+        quantize_weights(E, E + 1, shared_codes[:, T:])
         for s in range(len(SHARED)):
-            shared_expert(s, rows[s])
+            shared_expert(s, laid[s])
 
         result = keep.tile([P, T], F32, name="result")
 
-        def add_on_tensor(c, a, b, terms, total):
+        def add_on_tensor(c, terms, total):
+            width = total.shape[1]
             back_bank = banks[c % 3]
             sums = banks[3:6] if c % 2 == 0 else banks[6:8]
-            turned = keep.tile([P, b - a], F32, name="turned_%d" % a)
-            blocks = [slice(i, i + P) for i in range(0, b - a, P)]
+            turned = keep.tile([P, width], F32, name="turned_%d" % c)
+            blocks = [slice(i, i + P) for i in range(0, width, P)]
             for r, term in enumerate(terms):
                 for i, block in enumerate(blocks):
                     nc.tensor.matmul(
@@ -268,16 +256,14 @@ def tile_moe_shr_lin_none_kernel(tc, xT, w, gate, offs, pos1, pos2, pos3, out):
                 nc.scalar.copy(turned[:, block], sums[i][:, :P])
             for block in blocks:
                 nc.tensor.transpose(back_bank[:, block], turned[:, block], identity[:])
-            nc.scalar.copy(total, back_bank[:, : b - a])
+            nc.scalar.copy(total, back_bank[:, :width])
 
-        a, b = LAST_CHUNK
-        partial = keep.tile([P, b - a], F32, name="partial")
-        add_on_tensor(0, a, b, [ys[:, a:b]] + [fetch(r, a, b) for r in range(2)], partial[:])
-        for c, (a, b) in enumerate(OUT_CHUNKS):
-            add_on_tensor(c + 1, a, b, [ys[:, a:b]] + [fetch(r, a, b) for r in range(3)], result[:, a:b])
+        partial = keep.tile([P, VECTOR_TOKENS], F32, name="partial")
+        add_on_tensor(0, [ys[:, :VECTOR_TOKENS]] + [fetch(r, 0, VECTOR_TOKENS) for r in range(2)], partial[:])
+        for c, (a, b) in enumerate(TENSOR_CHUNKS):
+            add_on_tensor(c + 1, [ys[:, a:b]] + [fetch(r, a, b) for r in range(3)], result[:, a:b])
             nc.scalar.dma_start(out[:, a:b], result[:, a:b])
-        base = LAST_CHUNK[0]
-        last = [fetch(2, a, b) for a, b in LAST_PIECES]
-        for (a, b), term in zip(LAST_PIECES, last):
-            nc.vector.tensor_tensor(result[:, a:b], partial[:, a - base : b - base], term, ADD)
+        third_terms = [fetch(2, a, b) for a, b in VECTOR_PIECES]
+        for (a, b), term in zip(VECTOR_PIECES, third_terms):
+            nc.vector.tensor_tensor(result[:, a:b], partial[:, a:b], term, ADD)
             nc.sync.dma_start(out[:, a:b], result[:, a:b])

@@ -42,9 +42,11 @@ PRELOADED_WEIGHTS = (12, 13)
 GPSIMD_WEIGHTS = [(e, e + 2) for e in range(0, 12, 2)]
 SCALAR_WEIGHTS = [(13, 14), (14, 16)]
 
-VECTOR_TOKENS = 384
-VECTOR_PIECES = [(0, 256), (256, VECTOR_TOKENS)]
-TENSOR_CHUNKS = [(VECTOR_TOKENS, 640), (640, 896), (896, 1152), (1152, T)]
+VECTOR_TOKENS = BANK
+VECTOR_PIECES = [(0, 384), (384, VECTOR_TOKENS)]
+TENSOR_CHUNKS = [(VECTOR_TOKENS, 896), (896, 1152), (1152, T)]
+SCALAR_TERMS = [(2,), (2, 0), (2,), (2,)]
+SUMMED_VECTOR_TERMS = [(0,), (1,), (0, 1), (0, 1)]
 
 
 def tile_moe_shr_lin_none_kernel(tc, xT, w, gate, offs, pos1, pos2, pos3, out):
@@ -192,14 +194,25 @@ def tile_moe_shr_lin_none_kernel(tc, xT, w, gate, offs, pos1, pos2, pos3, out):
             a, b = SHARED[s]
             quantize_columns(count + s, rows, b - a)
             multiply(banks[s][:, : b - a], E, count + s, slice(0, b - a))
+
+        def empty_shared(s):
+            a, b = SHARED[s]
             nc.scalar.copy(ys[:, a:b], banks[s][:, : b - a])
 
-        def fetch(r, a, b):
-            term = keep.tile([P, b - a], F32, name="term_%d_%d" % (a, r))
+        def fetch_on_scalar(r, a, b, room):
+            raw = room[:, : b - a]
+            nc.scalar.activation(raw, y[:].indirect(places[r][:, a // STRIPE : b // STRIPE]), COPY)
+            return raw
+
+        def weigh(r, a, b, raw):
+            nc.vector.tensor_tensor(raw, raw, gates[r][:, a:b], MULT)
+            return raw
+
+        def fetch(r, a, b, term):
             nc.vector.tensor_tensor(
-                term[:], y[:].indirect(places[r][:, a // STRIPE : b // STRIPE]), gates[r][:, a:b], MULT
+                term, y[:].indirect(places[r][:, a // STRIPE : b // STRIPE]), gates[r][:, a:b], MULT
             )
-            return term[:]
+            return term
 
         round_weights_on_gpsimd(*PRELOADED_WEIGHTS)
         for a, b in LATE_CHUNKS:
@@ -223,47 +236,75 @@ def tile_moe_shr_lin_none_kernel(tc, xT, w, gate, offs, pos1, pos2, pos3, out):
         for g in range(count):
             interleave(g)
 
+        shared_codes = keep.tile([P, T + N], U32, name="shared_codes", tag="picked_1", align_bytes=64)
+        codes.extend(shared_codes[:, a:b] for a, b in SHARED)
         for g, (a, b) in enumerate(GROUPS):
+            if g == count - 1:
+                quantize_weights(E, E + 1, shared_codes[:, T:])
+                shared_expert(0, laid[0])
+                empty_shared(0)
             made = keep.tile([P, (b - a) // C * N], U32, name="w_codes_%d" % g, align_bytes=64)
             quantize_weights(a // C, b // C, made[:])
             experts(g)
 
-        shared_codes = keep.tile([P, T + N], U32, name="shared_codes", tag="picked_1", align_bytes=64)
-        codes.extend(shared_codes[:, a:b] for a, b in SHARED)
-        quantize_weights(E, E + 1, shared_codes[:, T:])
-        for s in range(len(SHARED)):
+        for s in range(1, len(SHARED)):
             shared_expert(s, laid[s])
 
         result = keep.tile([P, T], F32, name="result")
 
-        def add_on_tensor(c, terms, total):
-            width = total.shape[1]
-            back_bank = banks[c % 3]
-            sums = banks[3:6] if c % 2 == 0 else banks[6:8]
-            turned = keep.tile([P, width], F32, name="turned_%d" % c)
-            blocks = [slice(i, i + P) for i in range(0, width, P)]
+        def sum_bank(c):
+            return banks[3 + c % 4]
+
+        def blocks_of(width):
+            return [slice(i, i + P) for i in range(0, width, P)]
+
+        def add_up(c, terms):
+            blocks = blocks_of(terms[0].shape[1])
             for r, term in enumerate(terms):
                 for i, block in enumerate(blocks):
                     nc.tensor.matmul(
-                        sums[i][:, :P],
+                        sum_bank(c)[:, block],
                         term[:, block],
                         identity[:],
-                        start=r == 0,
-                        stop=r == len(terms) - 1,
+                        start=r == 0 and i == 0,
+                        stop=r == len(terms) - 1 and i == len(blocks) - 1,
                         is_transpose=True,
                     )
-            for i, block in enumerate(blocks):
-                nc.scalar.copy(turned[:, block], sums[i][:, :P])
-            for block in blocks:
-                nc.tensor.transpose(back_bank[:, block], turned[:, block], identity[:])
-            nc.scalar.copy(total, back_bank[:, :width])
 
-        partial = keep.tile([P, VECTOR_TOKENS], F32, name="partial")
-        add_on_tensor(0, [ys[:, :VECTOR_TOKENS]] + [fetch(r, 0, VECTOR_TOKENS) for r in range(2)], partial[:])
-        for c, (a, b) in enumerate(TENSOR_CHUNKS):
-            add_on_tensor(c + 1, [ys[:, a:b]] + [fetch(r, a, b) for r in range(3)], result[:, a:b])
+        def turn_back(c, width):
+            back_bank = banks[(0, 7, 1, 2)[c]]
+            turned = keep.tile([P, width], F32, name="turned_%d" % c)
+            nc.scalar.copy(turned[:], sum_bank(c)[:, :width])
+            for block in blocks_of(width):
+                nc.tensor.transpose(back_bank[:, block], turned[:, block], identity[:])
+            return back_bank
+
+        def store(a, b, back):
+            nc.scalar.copy(result[:, a:b], back[:, : b - a])
             nc.scalar.dma_start(out[:, a:b], result[:, a:b])
-        third_terms = [fetch(2, a, b) for a, b in VECTOR_PIECES]
-        for (a, b), term in zip(VECTOR_PIECES, third_terms):
-            nc.vector.tensor_tensor(result[:, a:b], partial[:, a:b], term, ADD)
+
+        chunks = [(0, VECTOR_TOKENS)] + TENSOR_CHUNKS
+        rooms = [w_raw[first][:].rearrange("p e j n -> p (e j n)") for first, last in GPSIMD_WEIGHTS]
+
+        def fresh(r, a, b):
+            return keep.tile([P, b - a], F32, name="term_%d_%d" % (a, r))[:]
+
+        for c, (a, b) in enumerate(chunks):
+            raws = [fetch_on_scalar(r, a, b, rooms[c][:, i * BANK :]) for i, r in enumerate(SCALAR_TERMS[c])]
+            if 0 < c < len(SHARED):
+                empty_shared(c)
+            fused = [fetch(r, a, b, fresh(r, a, b)) for r in SUMMED_VECTOR_TERMS[c]]
+            weighed = [weigh(r, a, b, raw) for r, raw in zip(SCALAR_TERMS[c], raws)]
+            add_up(c, [ys[:, a:b]] + fused + weighed)
+        backs = {}
+        for c in (1, 0):
+            backs[c] = turn_back(c, chunks[c][1] - chunks[c][0])
+        store(*chunks[1], backs[1])
+        for c in (2, 3):
+            backs[c] = turn_back(c, chunks[c][1] - chunks[c][0])
+        store(*chunks[2], backs[2])
+        store(*chunks[3], backs[3])
+        last_term = fetch(1, 0, VECTOR_TOKENS, fresh(1, 0, VECTOR_TOKENS))
+        for a, b in VECTOR_PIECES:
+            nc.vector.tensor_tensor(result[:, a:b], backs[0][:, a:b], last_term[:, a:b], ADD)
             nc.sync.dma_start(out[:, a:b], result[:, a:b])

@@ -42,11 +42,7 @@ PRELOADED_WEIGHTS = (12, 13)
 GPSIMD_WEIGHTS = [(e, e + 2) for e in range(0, 12, 2)]
 SCALAR_WEIGHTS = [(13, 14), (14, 16)]
 
-VECTOR_TOKENS = BANK
-VECTOR_PIECES = [(0, 384), (384, VECTOR_TOKENS)]
-TENSOR_CHUNKS = [(VECTOR_TOKENS, 896), (896, 1152), (1152, T)]
-SCALAR_TERMS = [(2,), (2, 0), (2,), (2,)]
-SUMMED_VECTOR_TERMS = [(0,), (1,), (0, 1), (0, 1)]
+FIRST, SECOND, THIRD, FOURTH, FIFTH = (0, 256), (256, 512), (512, 896), (896, 1152), (1152, T)
 
 
 def tile_moe_shr_lin_none_kernel(tc, xT, w, gate, offs, pos1, pos2, pos3, out):
@@ -252,59 +248,90 @@ def tile_moe_shr_lin_none_kernel(tc, xT, w, gate, offs, pos1, pos2, pos3, out):
 
         result = keep.tile([P, T], F32, name="result")
 
-        def sum_bank(c):
-            return banks[3 + c % 4]
-
-        def blocks_of(width):
-            return [slice(i, i + P) for i in range(0, width, P)]
-
-        def add_up(c, terms):
-            blocks = blocks_of(terms[0].shape[1])
-            for r, term in enumerate(terms):
-                for i, block in enumerate(blocks):
-                    nc.tensor.matmul(
-                        sum_bank(c)[:, block],
-                        term[:, block],
-                        identity[:],
-                        start=r == 0 and i == 0,
-                        stop=r == len(terms) - 1 and i == len(blocks) - 1,
-                        is_transpose=True,
-                    )
-
-        def turn_back(c, width):
-            back_bank = banks[(0, 7, 1, 2)[c]]
-            turned = keep.tile([P, width], F32, name="turned_%d" % c)
-            nc.scalar.copy(turned[:], sum_bank(c)[:, :width])
-            for block in blocks_of(width):
-                nc.tensor.transpose(back_bank[:, block], turned[:, block], identity[:])
-            return back_bank
-
-        def store(a, b, back):
-            nc.scalar.copy(result[:, a:b], back[:, : b - a])
-            nc.scalar.dma_start(out[:, a:b], result[:, a:b])
-
-        chunks = [(0, VECTOR_TOKENS)] + TENSOR_CHUNKS
         rooms = [w_raw[first][:].rearrange("p e j n -> p (e j n)") for first, last in GPSIMD_WEIGHTS]
+        chunks = [FIRST, SECOND, THIRD, FOURTH, FIFTH]
+        sums = {chunk: banks[3 + c % 4] for c, chunk in enumerate(chunks)}
+        backs = {chunk: banks[b] for chunk, b in zip(chunks, (0, 7, 1, 2, 0))}
+        passes_left = {(a, b): (3 if (a, b) in (THIRD, FOURTH) else 4) * (b - a) // P for a, b in chunks}
+        opened = set()
+
+        def add(chunk, term, a):
+            for i in range(0, term.shape[1], P):
+                passes_left[chunk] -= 1
+                column = a - chunk[0] + i
+                nc.tensor.matmul(
+                    sums[chunk][:, column : column + P],
+                    term[:, i : i + P],
+                    identity[:],
+                    start=chunk not in opened,
+                    stop=passes_left[chunk] == 0,
+                    is_transpose=True,
+                )
+                opened.add(chunk)
+
+        def turn_back(chunk, turned):
+            width = chunk[1] - chunk[0]
+            nc.scalar.copy(turned[:, :width], sums[chunk][:, :width])
+            for i in range(0, width, P):
+                nc.tensor.transpose(backs[chunk][:, i : i + P], turned[:, i : i + P], identity[:])
 
         def fresh(r, a, b):
             return keep.tile([P, b - a], F32, name="term_%d_%d" % (a, r))[:]
 
-        for c, (a, b) in enumerate(chunks):
-            raws = [fetch_on_scalar(r, a, b, rooms[c][:, i * BANK :]) for i, r in enumerate(SCALAR_TERMS[c])]
-            if 0 < c < len(SHARED):
-                empty_shared(c)
-            fused = [fetch(r, a, b, fresh(r, a, b)) for r in SUMMED_VECTOR_TERMS[c]]
-            weighed = [weigh(r, a, b, raw) for r, raw in zip(SCALAR_TERMS[c], raws)]
-            add_up(c, [ys[:, a:b]] + fused + weighed)
-        backs = {}
-        for c in (1, 0):
-            backs[c] = turn_back(c, chunks[c][1] - chunks[c][0])
-        store(*chunks[1], backs[1])
-        for c in (2, 3):
-            backs[c] = turn_back(c, chunks[c][1] - chunks[c][0])
-        store(*chunks[2], backs[2])
-        store(*chunks[3], backs[3])
-        last_term = fetch(1, 0, VECTOR_TOKENS, fresh(1, 0, VECTOR_TOKENS))
-        for a, b in VECTOR_PIECES:
-            nc.vector.tensor_tensor(result[:, a:b], backs[0][:, a:b], last_term[:, a:b], ADD)
+        def add_fused(chunk, r, a, b):
+            add(chunk, fetch(r, a, b, fresh(r, a, b)), a)
+
+        def add_weighed(chunk, r, a, b, raw):
+            add(chunk, weigh(r, a, b, raw), a)
+
+        def store(a, b):
+            nc.scalar.copy(result[:, a:b], backs[a, b][:, : b - a])
+            nc.scalar.dma_start(out[:, a:b], result[:, a:b])
+
+        def finish(chunk, term, a, b):
+            cols = slice(a - chunk[0], b - chunk[0])
+            nc.vector.tensor_tensor(result[:, a:b], backs[chunk][:, cols], term[:, cols], ADD)
             nc.sync.dma_start(out[:, a:b], result[:, a:b])
+
+        last_two = (FOURTH[0], T)
+        finished = (THIRD[0], FOURTH[1])
+        turned = keep.tile([P, T], F32, name="turned")
+
+        def turn(chunk):
+            turn_back(chunk, turned[:, chunk[0] : chunk[1]])
+
+        raws = {}
+        for c, chunk in enumerate((FIRST, SECOND)):
+            add(chunk, ys[:, chunk[0] : chunk[1]], chunk[0])
+            raws[chunk] = fetch_on_scalar(2, *chunk, rooms[c])
+            add_fused(chunk, 0, *chunk)
+            add_fused(chunk, 1, *chunk)
+            add_weighed(chunk, 2, *chunk, raws[chunk])
+        empty_shared(1)
+        empty_shared(2)
+        turn(FIRST)
+        raw_third = fetch_on_scalar(2, *THIRD, rooms[2])
+        raw_last = fetch_on_scalar(2, *last_two, rooms[3][:, 512:])
+        add(THIRD, ys[:, THIRD[0] : THIRD[1]], THIRD[0])
+        add(THIRD, fetch(0, *THIRD, fresh(0, *THIRD)), THIRD[0])
+        add_weighed(THIRD, 2, *THIRD, raw_third)
+        turn(SECOND)
+        store(*FIRST)
+        store(*SECOND)
+        add(FOURTH, ys[:, FOURTH[0] : FOURTH[1]], FOURTH[0])
+        add(FIFTH, ys[:, FIFTH[0] :], FIFTH[0])
+        term = fetch(0, *last_two, fresh(0, *last_two))
+        add(FOURTH, term[:, :256], FOURTH[0])
+        add(FIFTH, term[:, 256:], FIFTH[0])
+        add(FIFTH, fetch(1, *FIFTH, fresh(1, *FIFTH)), FIFTH[0])
+        weighed = fresh(2, *FOURTH)
+        nc.vector.tensor_tensor(weighed, raw_last[:, :256], gates[2][:, FOURTH[0] : FOURTH[1]], MULT)
+        add(FOURTH, weighed, FOURTH[0])
+        add_weighed(FIFTH, 2, *FIFTH, raw_last[:, 256:])
+        turn(THIRD)
+        turn(FOURTH)
+        turn(FIFTH)
+        store(*FIFTH)
+        last_term = fetch(1, *finished, rooms[3][:, 128:768])
+        finish(THIRD, last_term[:, :384], *THIRD)
+        finish(FOURTH, last_term[:, 384:], *FOURTH)

@@ -42,7 +42,8 @@ PRELOADED_WEIGHTS = (12, 13)
 GPSIMD_WEIGHTS = [(e, e + 2) for e in range(0, 12, 2)]
 SCALAR_WEIGHTS = [(13, 14), (14, 16)]
 
-FIRST, SECOND, THIRD, FOURTH, FIFTH = (0, 256), (256, 512), (512, 896), (896, 1152), (1152, T)
+FIRST, SECOND, THIRD, FOURTH = (0, 256), (256, 512), (512, 896), (896, T)
+LAST_CUT = 1152
 
 
 def tile_moe_shr_lin_none_kernel(tc, xT, w, gate, offs, pos1, pos2, pos3, out):
@@ -249,9 +250,9 @@ def tile_moe_shr_lin_none_kernel(tc, xT, w, gate, offs, pos1, pos2, pos3, out):
         result = keep.tile([P, T], F32, name="result")
 
         rooms = [w_raw[first][:].rearrange("p e j n -> p (e j n)") for first, last in GPSIMD_WEIGHTS]
-        chunks = [FIRST, SECOND, THIRD, FOURTH, FIFTH]
+        chunks = [FIRST, SECOND, THIRD, FOURTH]
         sums = {chunk: banks[3 + c % 4] for c, chunk in enumerate(chunks)}
-        backs = {chunk: banks[b] for chunk, b in zip(chunks, (0, 7, 1, 2, 0))}
+        backs = {chunk: banks[b] for chunk, b in zip(chunks, (0, 7, 1, 2))}
         passes_left = {(a, b): (3 if (a, b) in (THIRD, FOURTH) else 4) * (b - a) // P for a, b in chunks}
         opened = set()
 
@@ -293,45 +294,40 @@ def tile_moe_shr_lin_none_kernel(tc, xT, w, gate, offs, pos1, pos2, pos3, out):
             nc.vector.tensor_tensor(result[:, a:b], backs[chunk][:, cols], term[:, cols], ADD)
             nc.sync.dma_start(out[:, a:b], result[:, a:b])
 
-        last_two = (FOURTH[0], T)
-        finished = (THIRD[0], FOURTH[1])
         turned = keep.tile([P, T], F32, name="turned")
 
         def turn(chunk):
             turn_back(chunk, turned[:, chunk[0] : chunk[1]])
 
-        raws = {}
         for c, chunk in enumerate((FIRST, SECOND)):
             add(chunk, ys[:, chunk[0] : chunk[1]], chunk[0])
-            raws[chunk] = fetch_on_scalar(2, *chunk, rooms[c])
+            raw = fetch_on_scalar(2, *chunk, rooms[c])
             add_fused(chunk, 0, *chunk)
             add_fused(chunk, 1, *chunk)
-            add_weighed(chunk, 2, *chunk, raws[chunk])
+            add_weighed(chunk, 2, *chunk, raw)
         empty_shared(1)
         empty_shared(2)
-        turn(FIRST)
-        raw_third = fetch_on_scalar(2, *THIRD, rooms[2])
-        raw_last = fetch_on_scalar(2, *last_two, rooms[3][:, 512:])
-        add(THIRD, ys[:, THIRD[0] : THIRD[1]], THIRD[0])
-        add(THIRD, fetch(0, *THIRD, fresh(0, *THIRD)), THIRD[0])
-        add_weighed(THIRD, 2, *THIRD, raw_third)
-        turn(SECOND)
-        store(*FIRST)
-        store(*SECOND)
-        add(FOURTH, ys[:, FOURTH[0] : FOURTH[1]], FOURTH[0])
-        add(FIFTH, ys[:, FIFTH[0] :], FIFTH[0])
-        term = fetch(0, *last_two, fresh(0, *last_two))
-        add(FOURTH, term[:, :256], FOURTH[0])
-        add(FIFTH, term[:, 256:], FIFTH[0])
-        add(FIFTH, fetch(1, *FIFTH, fresh(1, *FIFTH)), FIFTH[0])
+        raws = [fetch_on_scalar(r, *THIRD, rooms[2][:, i * BANK :]) for i, r in enumerate((2, 0))]
+        raw_last = fetch_on_scalar(2, *FOURTH, rooms[3][:, 256:])
+        for chunk in (THIRD, FOURTH):
+            add(chunk, ys[:, chunk[0] : chunk[1]], chunk[0])
+        add_fused(FOURTH, 0, *FOURTH)
+        add_weighed(THIRD, 2, *THIRD, raws[0])
+        add_weighed(THIRD, 0, *THIRD, raws[1])
         weighed = fresh(2, *FOURTH)
-        nc.vector.tensor_tensor(weighed, raw_last[:, :256], gates[2][:, FOURTH[0] : FOURTH[1]], MULT)
-        add(FOURTH, weighed, FOURTH[0])
-        add_weighed(FIFTH, 2, *FIFTH, raw_last[:, 256:])
+        for a, b in ((0, 256), (256, 384)):
+            nc.vector.tensor_tensor(weighed[:, a:b], raw_last[:, a:b], gates[2][:, FOURTH[0] + a : FOURTH[0] + b], MULT)
+            add(FOURTH, weighed[:, a:b], FOURTH[0] + a)
+        turn(FIRST)
+        turn(SECOND)
         turn(THIRD)
+        store(*FIRST)
         turn(FOURTH)
-        turn(FIFTH)
-        store(*FIFTH)
-        last_term = fetch(1, *finished, rooms[3][:, 128:768])
-        finish(THIRD, last_term[:, :384], *THIRD)
-        finish(FOURTH, last_term[:, 384:], *FOURTH)
+        store(*SECOND)
+        last_third = fetch(1, *THIRD, rooms[3][:, :384])
+        last_fourth = rooms[3][:, 384:768]
+        fetch(1, FOURTH[0], LAST_CUT, last_fourth[:, :256])
+        finish(THIRD, last_third, *THIRD)
+        fetch(1, LAST_CUT, T, last_fourth[:, 256:])
+        finish(FOURTH, last_fourth, FOURTH[0], LAST_CUT)
+        finish(FOURTH, last_fourth, LAST_CUT, T)

@@ -42,7 +42,7 @@ PRELOADED_WEIGHTS = (12, 13)
 GPSIMD_WEIGHTS = [(e, e + 2) for e in range(0, 12, 2)]
 SCALAR_WEIGHTS = [(13, 14), (14, 16)]
 
-FIRST, SECOND, THIRD, FOURTH = (0, 256), (256, 512), (512, 896), (896, T)
+FIRST, SECOND, THIRD, FOURTH, FIFTH = (0, 256), (256, 512), (512, 768), (768, 1024), (1024, T)
 LAST_CUT = 1152
 
 
@@ -250,10 +250,10 @@ def tile_moe_shr_lin_none_kernel(tc, xT, w, gate, offs, pos1, pos2, pos3, out):
         result = keep.tile([P, T], F32, name="result")
 
         rooms = [w_raw[first][:].rearrange("p e j n -> p (e j n)") for first, last in GPSIMD_WEIGHTS]
-        chunks = [FIRST, SECOND, THIRD, FOURTH]
+        chunks = [FIRST, SECOND, THIRD, FOURTH, FIFTH]
         sums = {chunk: banks[3 + c % 4] for c, chunk in enumerate(chunks)}
-        backs = {chunk: banks[b] for chunk, b in zip(chunks, (0, 7, 1, 2))}
-        passes_left = {(a, b): (3 if (a, b) in (THIRD, FOURTH) else 4) * (b - a) // P for a, b in chunks}
+        backs = {chunk: banks[b] for chunk, b in zip(chunks, (0, 7, 1, 2, 0))}
+        passes_left = {(a, b): (3 if (a, b) in (THIRD, FOURTH, FIFTH) else 4) * (b - a) // P for a, b in chunks}
         opened = set()
 
         def add(chunk, term, a):
@@ -301,33 +301,37 @@ def tile_moe_shr_lin_none_kernel(tc, xT, w, gate, offs, pos1, pos2, pos3, out):
 
         for c, chunk in enumerate((FIRST, SECOND)):
             add(chunk, ys[:, chunk[0] : chunk[1]], chunk[0])
-            raw = fetch_on_scalar(2, *chunk, rooms[c])
+            raw = fetch_on_scalar(2, *chunk, rooms[c][:, 256:])
             add_fused(chunk, 0, *chunk)
             add_fused(chunk, 1, *chunk)
             add_weighed(chunk, 2, *chunk, raw)
         empty_shared(1)
-        empty_shared(2)
         raws = [fetch_on_scalar(r, *THIRD, rooms[2][:, i * BANK :]) for i, r in enumerate((2, 0))]
-        raw_last = fetch_on_scalar(2, *FOURTH, rooms[3][:, 256:])
+        raw_fourth = fetch_on_scalar(2, *FOURTH, rooms[3])
         for chunk in (THIRD, FOURTH):
             add(chunk, ys[:, chunk[0] : chunk[1]], chunk[0])
-        add_fused(FOURTH, 0, *FOURTH)
         add_weighed(THIRD, 2, *THIRD, raws[0])
         add_weighed(THIRD, 0, *THIRD, raws[1])
-        weighed = fresh(2, *FOURTH)
-        for a, b in ((0, 256), (256, 384)):
-            nc.vector.tensor_tensor(weighed[:, a:b], raw_last[:, a:b], gates[2][:, FOURTH[0] + a : FOURTH[0] + b], MULT)
-            add(FOURTH, weighed[:, a:b], FOURTH[0] + a)
+        empty_shared(2)
         turn(FIRST)
         turn(SECOND)
+        add_fused(FOURTH, 0, *FOURTH)
+        add_weighed(FOURTH, 2, *FOURTH, raw_fourth)
+        raw_last = fetch_on_scalar(2, *FIFTH, rooms[1][:, 448:])
         turn(THIRD)
+        add(FIFTH, ys[:, FIFTH[0] :], FIFTH[0])
+        add_fused(FIFTH, 0, *FIFTH)
+        weighed = fresh(2, *FIFTH)
+        for a in (0, P):
+            nc.vector.tensor_tensor(weighed[:, a : a + P], raw_last[:, a : a + P], gates[2][:, FIFTH[0] + a : FIFTH[0] + a + P], MULT)
+            add(FIFTH, weighed[:, a : a + P], FIFTH[0] + a)
         store(*FIRST)
         turn(FOURTH)
         store(*SECOND)
-        last_third = fetch(1, *THIRD, rooms[3][:, :384])
-        last_fourth = rooms[3][:, 384:768]
-        fetch(1, FOURTH[0], LAST_CUT, last_fourth[:, :256])
-        finish(THIRD, last_third, *THIRD)
-        fetch(1, LAST_CUT, T, last_fourth[:, 256:])
-        finish(FOURTH, last_fourth, FOURTH[0], LAST_CUT)
-        finish(FOURTH, last_fourth, LAST_CUT, T)
+        turn(FIFTH)
+        last_two = fetch(1, THIRD[0], FOURTH[1], rooms[1][:, :512])
+        last_fifth = fetch(1, *FIFTH, rooms[1][:, 512:768])
+        finish(THIRD, last_two[:, :256], *THIRD)
+        finish(FOURTH, last_two[:, 256:], *FOURTH)
+        finish(FIFTH, last_fifth, FIFTH[0], LAST_CUT)
+        finish(FIFTH, last_fifth, LAST_CUT, T)

@@ -251,8 +251,8 @@ def tile_moe_shr_lin_none_kernel(tc, xT, w, gate, offs, pos1, pos2, pos3, out):
 
         rooms = [w_raw[first][:].rearrange("p e j n -> p (e j n)") for first, last in GPSIMD_WEIGHTS]
         chunks = [FIRST, SECOND, THIRD, FOURTH, FIFTH]
-        sums = {chunk: banks[3 + c % 4] for c, chunk in enumerate(chunks)}
-        backs = {chunk: banks[b] for chunk, b in zip(chunks, (0, 7, 1, 2, 0))}
+        sums = {chunk: banks[3 + c] for c, chunk in enumerate(chunks)}
+        backs = {chunk: banks[b] for chunk, b in zip(chunks, (0, 1, 2, 3, 4))}
         passes_left = {(a, b): (3 if (a, b) in (THIRD, FOURTH, FIFTH) else 4) * (b - a) // P for a, b in chunks}
         opened = set()
 
@@ -299,38 +299,45 @@ def tile_moe_shr_lin_none_kernel(tc, xT, w, gate, offs, pos1, pos2, pos3, out):
         def turn(chunk):
             turn_back(chunk, turned[:, chunk[0] : chunk[1]])
 
-        for c, chunk in enumerate((FIRST, SECOND)):
+        def add_ys(chunk):
             add(chunk, ys[:, chunk[0] : chunk[1]], chunk[0])
-            raw = fetch_on_scalar(2, *chunk, rooms[c][:, 256:])
-            add_fused(chunk, 0, *chunk)
-            add_fused(chunk, 1, *chunk)
-            add_weighed(chunk, 2, *chunk, raw)
+
+        room = keep.tile([P, 2 * SPAN], F32, name="room", tag="picked_0", align_bytes=64)
+        add_ys(FIRST)
+        add_ys(SECOND)
         empty_shared(1)
-        raws = [fetch_on_scalar(r, *THIRD, rooms[2][:, i * BANK :]) for i, r in enumerate((2, 0))]
-        raw_fourth = fetch_on_scalar(2, *FOURTH, rooms[3])
-        for chunk in (THIRD, FOURTH):
-            add(chunk, ys[:, chunk[0] : chunk[1]], chunk[0])
-        add_weighed(THIRD, 2, *THIRD, raws[0])
-        add_weighed(THIRD, 0, *THIRD, raws[1])
+        add_ys(THIRD)
+        add_ys(FOURTH)
+        add_fused(FIRST, 0, *FIRST)
+        add_fused(FIRST, 1, *FIRST)
+        add(FIRST, fetch(2, *FIRST, room[:, 832:1088]), FIRST[0])
+        raw_second = fetch_on_scalar(2, *SECOND, rooms[2])
+        raw_third = fetch_on_scalar(2, *THIRD, rooms[2][:, 256:])
         empty_shared(2)
+        add_ys(FIFTH)
+        raw_third_0 = fetch_on_scalar(0, *THIRD, rooms[2][:, 512:])
+        add_weighed(SECOND, 2, *SECOND, raw_second)
+        add_fused(SECOND, 0, *SECOND)
+        add_weighed(THIRD, 2, *THIRD, raw_third)
         turn(FIRST)
-        turn(SECOND)
-        add_fused(FOURTH, 0, *FOURTH)
-        add_weighed(FOURTH, 2, *FOURTH, raw_fourth)
-        raw_last = fetch_on_scalar(2, *FIFTH, rooms[1][:, 448:])
-        turn(THIRD)
-        add(FIFTH, ys[:, FIFTH[0] :], FIFTH[0])
+        raw_fourth_0 = fetch_on_scalar(0, *FOURTH, room[:, 1024:])
+        raw_last = fetch_on_scalar(2, FOURTH[0], T, room[:, 512:])
+        add_fused(SECOND, 1, *SECOND)
+        add_weighed(THIRD, 0, *THIRD, raw_third_0)
         add_fused(FIFTH, 0, *FIFTH)
-        weighed = fresh(2, *FIFTH)
-        for a in (0, P):
-            nc.vector.tensor_tensor(weighed[:, a : a + P], raw_last[:, a : a + P], gates[2][:, FIFTH[0] + a : FIFTH[0] + a + P], MULT)
-            add(FIFTH, weighed[:, a : a + P], FIFTH[0] + a)
+        turn(SECOND)
+        add_weighed(FOURTH, 0, *FOURTH, raw_fourth_0)
+        for a, b in (FOURTH, FIFTH):
+            weighed = fresh(2, a, b)
+            nc.vector.tensor_tensor(weighed, raw_last[:, a - FOURTH[0] : b - FOURTH[0]], gates[2][:, a:b], MULT)
+            add((a, b), weighed, a)
+        turn(THIRD)
         store(*FIRST)
         turn(FOURTH)
-        store(*SECOND)
         turn(FIFTH)
-        last_two = fetch(1, THIRD[0], FOURTH[1], rooms[1][:, :512])
-        last_fifth = fetch(1, *FIFTH, rooms[1][:, 512:768])
+        store(*SECOND)
+        last_two = fetch(1, THIRD[0], FOURTH[1], room[:, 256:768])
+        last_fifth = fetch(1, *FIFTH, room[:, 768:1024])
         finish(THIRD, last_two[:, :256], *THIRD)
         finish(FOURTH, last_two[:, 256:], *FOURTH)
         finish(FIFTH, last_fifth, FIFTH[0], LAST_CUT)

@@ -42,8 +42,19 @@ PRELOADED_WEIGHTS = (12, 13)
 GPSIMD_WEIGHTS = [(e, e + 2) for e in range(0, 12, 2)]
 SCALAR_WEIGHTS = [(13, 14), (14, 16)]
 
-FIRST, SECOND, THIRD, FOURTH, FIFTH = (0, 256), (256, 512), (512, 768), (768, 1024), (1024, T)
-LAST_CUT = 1152
+CHUNK = 256
+CHUNKS = [(a, a + CHUNK) for a in range(0, T, CHUNK)]
+FIRST, SECOND, THIRD, FOURTH, FIFTH = CHUNKS
+WHOLLY_SUMMED = (FIRST, SECOND)
+LAST_CUT = T - P
+FIRST_SUM_BANK = len(SHARED)
+
+RELAY_SEAM = 4 * CHUNK
+RELAY_FIRST_TERM = slice(RELAY_SEAM + P // 2 - CHUNK, RELAY_SEAM + P // 2)
+RELAY_TERM_2 = slice(RELAY_SEAM - 2 * CHUNK, RELAY_SEAM)
+RELAY_TERM_0 = slice(RELAY_SEAM, RELAY_SEAM + CHUNK)
+RELAY_LAST_TWO = slice(RELAY_SEAM - 3 * CHUNK, RELAY_SEAM - CHUNK)
+RELAY_LAST_ONE = slice(RELAY_SEAM - CHUNK, RELAY_SEAM)
 
 
 def tile_moe_shr_lin_none_kernel(tc, xT, w, gate, offs, pos1, pos2, pos3, out):
@@ -196,19 +207,19 @@ def tile_moe_shr_lin_none_kernel(tc, xT, w, gate, offs, pos1, pos2, pos3, out):
             a, b = SHARED[s]
             nc.scalar.copy(ys[:, a:b], banks[s][:, : b - a])
 
-        def fetch_on_scalar(r, a, b, room):
-            raw = room[:, : b - a]
-            nc.scalar.activation(raw, y[:].indirect(places[r][:, a // STRIPE : b // STRIPE]), COPY)
-            return raw
+        def slot_results(r, a, b):
+            return y[:].indirect(places[r][:, a // STRIPE : b // STRIPE])
 
-        def weigh(r, a, b, raw):
-            nc.vector.tensor_tensor(raw, raw, gates[r][:, a:b], MULT)
-            return raw
+        def fetch_term(r, a, b, term):
+            nc.vector.tensor_tensor(term, slot_results(r, a, b), gates[r][:, a:b], MULT)
+            return term
 
-        def fetch(r, a, b, term):
-            nc.vector.tensor_tensor(
-                term, y[:].indirect(places[r][:, a // STRIPE : b // STRIPE]), gates[r][:, a:b], MULT
-            )
+        def fetch_plain(r, a, b, plain):
+            nc.scalar.activation(plain, slot_results(r, a, b), COPY)
+            return plain
+
+        def weigh(r, a, b, plain, term):
+            nc.vector.tensor_tensor(term, plain, gates[r][:, a:b], MULT)
             return term
 
         round_weights_on_gpsimd(*PRELOADED_WEIGHTS)
@@ -248,97 +259,89 @@ def tile_moe_shr_lin_none_kernel(tc, xT, w, gate, offs, pos1, pos2, pos3, out):
             shared_expert(s, laid[s])
 
         result = keep.tile([P, T], F32, name="result")
+        turned = keep.tile([P, T], F32, name="turned")
+        relay = keep.tile([P, 2 * SPAN], F32, name="relay", tag="picked_0", align_bytes=64)
+        spent = w_raw[GPSIMD_WEIGHTS[2][0]][:].rearrange("p e j n -> p (e j n)")
+        sums = {chunk: banks[FIRST_SUM_BANK + c] for c, chunk in enumerate(CHUNKS)}
+        backs = {chunk: banks[c] for c, chunk in enumerate(CHUNKS)}
+        summands = {chunk: 4 if chunk in WHOLLY_SUMMED else 3 for chunk in CHUNKS}
+        added = {chunk: 0 for chunk in CHUNKS}
+        blocks = [slice(i, i + P) for i in range(0, CHUNK, P)]
 
-        rooms = [w_raw[first][:].rearrange("p e j n -> p (e j n)") for first, last in GPSIMD_WEIGHTS]
-        chunks = [FIRST, SECOND, THIRD, FOURTH, FIFTH]
-        sums = {chunk: banks[3 + c] for c, chunk in enumerate(chunks)}
-        backs = {chunk: banks[b] for chunk, b in zip(chunks, (0, 1, 2, 3, 4))}
-        passes_left = {(a, b): (3 if (a, b) in (THIRD, FOURTH, FIFTH) else 4) * (b - a) // P for a, b in chunks}
-        opened = set()
-
-        def add(chunk, term, a):
-            for i in range(0, term.shape[1], P):
-                passes_left[chunk] -= 1
-                column = a - chunk[0] + i
+        def add(chunk, term):
+            for i, block in enumerate(blocks):
                 nc.tensor.matmul(
-                    sums[chunk][:, column : column + P],
-                    term[:, i : i + P],
+                    sums[chunk][:, block],
+                    term[:, block],
                     identity[:],
-                    start=chunk not in opened,
-                    stop=passes_left[chunk] == 0,
+                    start=added[chunk] == 0 and i == 0,
+                    stop=added[chunk] == summands[chunk] - 1 and i == len(blocks) - 1,
                     is_transpose=True,
                 )
-                opened.add(chunk)
+            added[chunk] = added[chunk] + 1
 
-        def turn_back(chunk, turned):
-            width = chunk[1] - chunk[0]
-            nc.scalar.copy(turned[:, :width], sums[chunk][:, :width])
-            for i in range(0, width, P):
-                nc.tensor.transpose(backs[chunk][:, i : i + P], turned[:, i : i + P], identity[:])
+        def add_shared(chunk):
+            add(chunk, ys[:, chunk[0] : chunk[1]])
 
-        def fresh(r, a, b):
-            return keep.tile([P, b - a], F32, name="term_%d_%d" % (a, r))[:]
+        def new_term(r, chunk):
+            return keep.tile([P, CHUNK], F32, name="term_%d_%d" % (chunk[0], r))[:]
 
-        def add_fused(chunk, r, a, b):
-            add(chunk, fetch(r, a, b, fresh(r, a, b)), a)
+        def add_fetched(chunk, r):
+            add(chunk, fetch_term(r, *chunk, new_term(r, chunk)))
 
-        def add_weighed(chunk, r, a, b, raw):
-            add(chunk, weigh(r, a, b, raw), a)
+        def add_weighed_in_place(chunk, r, plain):
+            add(chunk, weigh(r, *chunk, plain, plain))
 
-        def store(a, b):
-            nc.scalar.copy(result[:, a:b], backs[a, b][:, : b - a])
-            nc.scalar.dma_start(out[:, a:b], result[:, a:b])
+        def turn_back(chunk):
+            rows = turned[:, chunk[0] : chunk[1]]
+            nc.scalar.copy(rows, sums[chunk][:, :CHUNK])
+            for block in blocks:
+                nc.tensor.transpose(backs[chunk][:, block], rows[:, block], identity[:])
+
+        def store(chunk):
+            a, b = chunk
+            nc.scalar.copy(result[:, a:b], backs[chunk][:, :CHUNK])
+            nc.sync.dma_start(out[:, a:b], result[:, a:b])
 
         def finish(chunk, term, a, b):
             cols = slice(a - chunk[0], b - chunk[0])
             nc.vector.tensor_tensor(result[:, a:b], backs[chunk][:, cols], term[:, cols], ADD)
             nc.sync.dma_start(out[:, a:b], result[:, a:b])
 
-        turned = keep.tile([P, T], F32, name="turned")
-
-        def turn(chunk):
-            turn_back(chunk, turned[:, chunk[0] : chunk[1]])
-
-        def add_ys(chunk):
-            add(chunk, ys[:, chunk[0] : chunk[1]], chunk[0])
-
-        room = keep.tile([P, 2 * SPAN], F32, name="room", tag="picked_0", align_bytes=64)
-        add_ys(FIRST)
-        add_ys(SECOND)
+        add_shared(FIRST)
+        add_shared(SECOND)
         empty_shared(1)
-        add_ys(THIRD)
-        add_ys(FOURTH)
-        add_fused(FIRST, 0, *FIRST)
-        add_fused(FIRST, 1, *FIRST)
-        add(FIRST, fetch(2, *FIRST, room[:, 832:1088]), FIRST[0])
-        raw_second = fetch_on_scalar(2, *SECOND, rooms[2])
-        raw_third = fetch_on_scalar(2, *THIRD, rooms[2][:, 256:])
+        add_shared(THIRD)
+        add_shared(FOURTH)
+        add_fetched(FIRST, 0)
+        add_fetched(FIRST, 1)
+        add(FIRST, fetch_term(2, *FIRST, relay[:, RELAY_FIRST_TERM]))
+        second_2 = fetch_plain(2, *SECOND, spent[:, :CHUNK])
+        third_2 = fetch_plain(2, *THIRD, spent[:, CHUNK : 2 * CHUNK])
         empty_shared(2)
-        add_ys(FIFTH)
-        raw_third_0 = fetch_on_scalar(0, *THIRD, rooms[2][:, 512:])
-        add_weighed(SECOND, 2, *SECOND, raw_second)
-        add_fused(SECOND, 0, *SECOND)
-        add_weighed(THIRD, 2, *THIRD, raw_third)
-        turn(FIRST)
-        raw_fourth_0 = fetch_on_scalar(0, *FOURTH, room[:, 1024:])
-        raw_last = fetch_on_scalar(2, FOURTH[0], T, room[:, 512:])
-        add_fused(SECOND, 1, *SECOND)
-        add_weighed(THIRD, 0, *THIRD, raw_third_0)
-        add_fused(FIFTH, 0, *FIFTH)
-        turn(SECOND)
-        add_weighed(FOURTH, 0, *FOURTH, raw_fourth_0)
-        for a, b in (FOURTH, FIFTH):
-            weighed = fresh(2, a, b)
-            nc.vector.tensor_tensor(weighed, raw_last[:, a - FOURTH[0] : b - FOURTH[0]], gates[2][:, a:b], MULT)
-            add((a, b), weighed, a)
-        turn(THIRD)
-        store(*FIRST)
-        turn(FOURTH)
-        turn(FIFTH)
-        store(*SECOND)
-        last_two = fetch(1, THIRD[0], FOURTH[1], room[:, 256:768])
-        last_fifth = fetch(1, *FIFTH, room[:, 768:1024])
-        finish(THIRD, last_two[:, :256], *THIRD)
-        finish(FOURTH, last_two[:, 256:], *FOURTH)
-        finish(FIFTH, last_fifth, FIFTH[0], LAST_CUT)
-        finish(FIFTH, last_fifth, LAST_CUT, T)
+        add_shared(FIFTH)
+        third_0 = fetch_plain(0, *THIRD, spent[:, 2 * CHUNK : 3 * CHUNK])
+        add_weighed_in_place(SECOND, 2, second_2)
+        add_fetched(SECOND, 0)
+        add_weighed_in_place(THIRD, 2, third_2)
+        turn_back(FIRST)
+        fourth_0 = fetch_plain(0, *FOURTH, relay[:, RELAY_TERM_0])
+        last_2 = fetch_plain(2, FOURTH[0], FIFTH[1], relay[:, RELAY_TERM_2])
+        add_fetched(SECOND, 1)
+        add_weighed_in_place(THIRD, 0, third_0)
+        add_fetched(FIFTH, 0)
+        turn_back(SECOND)
+        add_weighed_in_place(FOURTH, 0, fourth_0)
+        add(FOURTH, weigh(2, *FOURTH, last_2[:, :CHUNK], new_term(2, FOURTH)))
+        add(FIFTH, weigh(2, *FIFTH, last_2[:, CHUNK:], new_term(2, FIFTH)))
+        turn_back(THIRD)
+        store(FIRST)
+        turn_back(FOURTH)
+        turn_back(FIFTH)
+        store(SECOND)
+        middle_1 = fetch_term(1, THIRD[0], FOURTH[1], relay[:, RELAY_LAST_TWO])
+        fifth_1 = fetch_term(1, *FIFTH, relay[:, RELAY_LAST_ONE])
+        finish(THIRD, middle_1[:, :CHUNK], *THIRD)
+        finish(FOURTH, middle_1[:, CHUNK:], *FOURTH)
+        finish(FIFTH, fifth_1, FIFTH[0], LAST_CUT)
+        finish(FIFTH, fifth_1, LAST_CUT, T)

from contextlib import ExitStack

import concourse.mybir as mybir
from concourse.masks import make_identity

K, T, E, C, N = 512, 1280, 15, 256, 128
SLOTS = E * C
FLOPS = 2 * K * N * (SLOTS + T)

F32 = mybir.dt.float32
BF16 = mybir.dt.bfloat16
U32 = mybir.dt.uint32
U16 = mybir.dt.uint16
U8 = mybir.dt.uint8
FP8X4 = mybir.dt.float8_e4m3fn_x4
MULT = mybir.AluOpType.mult
ADD = mybir.AluOpType.add
COPY = mybir.ActivationFunctionType.Copy

P = 128
PACK = 4
STRIPE = 16
BANK = 512
BANKS = 8
EARLY, LATE = 1, 0

EARLY_CHUNKS = [(0, 512), (512, 768), (768, 1024), (1024, 1152), (1152, 1280)]
LATE_CHUNKS = [(1024, 1280), (512, 1024), (0, 512)]

GROUPS = [(s, min(s + BANK, SLOTS)) for s in range(0, SLOTS, BANK)]
SHARED = [(s, min(s + BANK, T)) for s in range(0, T, BANK)]
CODE_TILES = 4

SCALAR_SLOTS = 960
SPAN = 4 * BANK
SECOND_MIDDLE = (SPAN + SLOTS) // 2
EARLY_RUNS = [(SCALAR_SLOTS, SPAN), (SPAN, SECOND_MIDDLE), (SECOND_MIDDLE, SLOTS)]
LATE_RUNS = [(0, SPAN // 2), (SPAN // 2, SPAN), (SPAN, SECOND_MIDDLE), (SECOND_MIDDLE, SLOTS)]
WINDOW = T + 176

PRELOADED_WEIGHTS = (12, 13)
GPSIMD_WEIGHTS = [(e, e + 2) for e in range(0, 12, 2)]
SCALAR_WEIGHTS = [(13, 14), (14, 16)]

CHUNK = 256
CHUNKS = [(a, a + CHUNK) for a in range(0, T, CHUNK)]
FIRST, SECOND, THIRD, FOURTH, FIFTH = CHUNKS
WHOLLY_SUMMED = (FIRST, SECOND)
LAST_CUT = T - P
FIRST_SUM_BANK = len(SHARED)

RELAY_SEAM = 4 * CHUNK
RELAY_FIRST_TERM = slice(RELAY_SEAM + P // 2 - CHUNK, RELAY_SEAM + P // 2)
RELAY_TERM_2 = slice(RELAY_SEAM - 2 * CHUNK, RELAY_SEAM)
RELAY_TERM_0 = slice(RELAY_SEAM, RELAY_SEAM + CHUNK)
RELAY_LAST_TWO = slice(RELAY_SEAM - 3 * CHUNK, RELAY_SEAM - CHUNK)
RELAY_LAST_ONE = slice(RELAY_SEAM - CHUNK, RELAY_SEAM)


def tile_moe_shr_lin_none_kernel(tc, xT, w, gate, offs, pos1, pos2, pos3, out):
    nc = tc.nc
    count = len(GROUPS)
    with ExitStack() as ctx:
        keep = ctx.enter_context(tc.tile_pool(name="keep", bufs=1))
        psum = ctx.enter_context(tc.psum_pool(name="psum", bufs=1))

        x_rows = xT.rearrange("(p h j) t -> p h j t", h=2, j=2)
        x_raw = {}
        w_raw = {}
        offsets = keep.tile([P, SLOTS // STRIPE], U16, name="offsets")

        def load_x(h, chunks):
            for a, b in chunks:
                x_raw[h, a] = keep.tile([P, 2, b - a], F32, name="x_raw_%d_%d" % (h, a), align_bytes=64)
                nc.sync.dma_start(x_raw[h, a][:], x_rows[:, h, :, a:b])

        def load_w(first, last):
            w_raw[first] = keep.tile([P, last - first, PACK, N], F32, name="w_raw_%d" % first)
            nc.sync.dma_start(w_raw[first][:], w[first:last].rearrange("e (p j) n -> p e j n", j=PACK))

        load_x(EARLY, EARLY_CHUNKS)
        nc.sync.dma_start(offsets[:], offs)
        load_w(*PRELOADED_WEIGHTS)
        load_x(LATE, LATE_CHUNKS)
        for first, last in GPSIMD_WEIGHTS + SCALAR_WEIGHTS:
            load_w(first, last)
        places = []
        gates = []
        for r, pos in enumerate((pos1, pos2, pos3)):
            places.append(keep.tile([P, T // STRIPE], U16, name="places_%d" % r))
            nc.sync.dma_start(places[r][:], pos)
        for r in range(3):
            gates.append(keep.tile([P, T], F32, name="gates_%d" % r))
            nc.sync.dma_start(gates[r][:], gate[r])

        identity = keep.tile([P, P], F32, name="identity")
        make_identity(nc, identity[:])

        x_both = keep.tile([P, 2 * (T + WINDOW)], BF16, name="x_both", align_bytes=64)
        nc.vector.memset(x_both[:, 4 * T :], 0.0)
        x_pairs = [x_both[:, 2 * T * h : 2 * T * (h + 1)].rearrange("p (t j) -> p t j", j=2) for h in range(2)]
        x_planes = [keep.tile([P, T], BF16, name="x_plane_%d" % j) for j in range(2)]
        for a, b in EARLY_CHUNKS:
            nc.vector.tensor_copy(x_pairs[EARLY][:, a:b, :], x_raw[EARLY, a][:].rearrange("p j t -> p t j"))
            for j in range(2):
                nc.scalar.copy(x_planes[j][:, a:b], x_raw[EARLY, a][:, j, :])
        x_words = x_both[:].bitcast(U32)
        x_halves = x_words[:, : 2 * T].bitcast(F32).rearrange("p (h t) -> p t h", h=2)

        banks = [psum.tile([P, BANK], F32, name="bank_%d" % i) for i in range(BANKS)]
        picked = [
            keep.tile([P, 2 * SPAN], U32, name="picked_%d" % i, tag="picked_%d" % i, align_bytes=64) for i in range(2)
        ]
        grouped = [keep.tile([P, 2 * BANK], F32, name="grouped_%d" % i, align_bytes=64) for i in range(count)]
        ring = [keep.tile([P, BANK], U32, name="codes_%d" % i, align_bytes=64) for i in range(CODE_TILES)]
        codes = [ring[i % CODE_TILES] for i in range(count)]
        scales = [keep.tile([P, BANK], U8, name="scales_%d" % i, align_bytes=64) for i in range(CODE_TILES)]
        w_grouped = keep.tile([P, E + 1, N, PACK], BF16, name="w_grouped", align_bytes=64)
        w_scales = keep.tile([P, (E + 1) * N], U8, name="w_scales", align_bytes=64)
        w_codes = {}
        singles = keep.tile([P, 2 * SCALAR_SLOTS], BF16, name="singles")
        y = keep.tile([P, SLOTS], F32, name="y")
        ys = keep.tile([P, T], F32, name="ys")

        def gather_pairs(h, a, b):
            start = h * SPAN + a % SPAN
            nc.vector.tensor_copy(
                picked[a // SPAN][:, start : start + b - a],
                x_words[:, h * T : h * T + WINDOW].indirect(offsets[:, a // STRIPE : b // STRIPE]),
            )

        def gather_values(j, a, b):
            nc.scalar.activation(
                singles[:, j * SCALAR_SLOTS + a : j * SCALAR_SLOTS + b],
                x_planes[j][:].indirect(offsets[:, a // STRIPE : b // STRIPE]),
                COPY,
            )

        def interleave(g):
            a, b = GROUPS[g]
            halves = picked[a // SPAN][:].bitcast(F32).rearrange("p (h s) -> p s h", h=2)
            nc.scalar.copy(
                grouped[g][:, : 2 * (b - a)].rearrange("p (s h) -> p s h", h=2),
                halves[:, a % SPAN : a % SPAN + b - a, :],
            )

        def round_weights_on_scalar(first, last):
            for e in range(first, last):
                nc.scalar.copy(
                    w_grouped[:, e].rearrange("p (c i) j -> p c j i", i=4),
                    w_raw[first][:, e - first].rearrange("p j (c i) -> p c j i", i=4),
                )

        def round_on_gpsimd(rounded, raw):
            nc.gpsimd.tensor_scalar(rounded, raw, 1.0, 0.0, MULT, ADD)

        def round_weights_on_gpsimd(first, last):
            round_on_gpsimd(w_grouped[:, first:last], w_raw[first][:].rearrange("p e j n -> p e n j"))

        def quantize_weights(first, last, made):
            for e in range(first, last):
                w_codes[e] = made[:, (e - first) * N : (e - first + 1) * N]
            nc.vector.quantize_mx(
                out=made.bitcast(FP8X4),
                scales=w_scales[:, first * N : last * N],
                in_=w_grouped[:, first:last].rearrange("p e n j -> p (e n j)"),
            )

        def quantize_columns(i, source, width):
            nc.vector.quantize_mx(
                out=codes[i][:, :width].bitcast(FP8X4),
                scales=scales[i % CODE_TILES][:, :width],
                in_=source[:, : 2 * width].bitcast(BF16),
            )

        def multiply(acc, e, i, cols):
            nc.tensor.matmul_mx(
                out=acc,
                lhsT=w_codes[e].bitcast(FP8X4),
                lhsT_scale=w_scales[:, e * N : (e + 1) * N],
                rhs=codes[i][:, cols].bitcast(FP8X4),
                rhs_scale=scales[i % CODE_TILES][:, cols],
                start=True,
                stop=True,
            )

        def experts(g):
            a, b = GROUPS[g]
            quantize_columns(g, grouped[g], b - a)
            for e in range(a // C, b // C):
                cols = slice(e * C - a, (e + 1) * C - a)
                multiply(banks[g][:, cols], e, g, cols)
            nc.scalar.copy(y[:, a:b], banks[g][:, : b - a])

        def lay_tokens(s):
            a, b = SHARED[s]
            rows = x_raw[LATE, a][:].rearrange("p j t -> p (j t)")
            nc.scalar.copy(rows.rearrange("p (t h) -> p t h", h=2), x_halves[:, a:b, :])
            return rows

        def shared_expert(s, rows):
            a, b = SHARED[s]
            quantize_columns(count + s, rows, b - a)
            multiply(banks[s][:, : b - a], E, count + s, slice(0, b - a))

        def empty_shared(s):
            a, b = SHARED[s]
            nc.scalar.copy(ys[:, a:b], banks[s][:, : b - a])

        def slot_results(r, a, b):
            return y[:].indirect(places[r][:, a // STRIPE : b // STRIPE])

        def fetch_term(r, a, b, term):
            nc.vector.tensor_tensor(term, slot_results(r, a, b), gates[r][:, a:b], MULT)
            return term

        def fetch_plain(r, a, b, plain):
            nc.scalar.activation(plain, slot_results(r, a, b), COPY)
            return plain

        def weigh(r, a, b, plain, term):
            nc.vector.tensor_tensor(term, plain, gates[r][:, a:b], MULT)
            return term

        round_weights_on_gpsimd(*PRELOADED_WEIGHTS)
        for a, b in LATE_CHUNKS:
            round_on_gpsimd(x_pairs[LATE][:, a:b, :], x_raw[LATE, a][:].rearrange("p j t -> p t j"))
        for first, last in GPSIMD_WEIGHTS:
            round_weights_on_gpsimd(first, last)
        for j in range(2):
            gather_values(j, 0, BANK)
            gather_values(j, BANK, SCALAR_SLOTS)
        nc.scalar.copy(
            picked[0][:, EARLY * SPAN : EARLY * SPAN + SCALAR_SLOTS].bitcast(BF16).rearrange("p (s j) -> p s j", j=2),
            singles[:].rearrange("p (j s) -> p s j", j=2),
        )
        for a, b in EARLY_RUNS:
            gather_pairs(EARLY, a, b)
        for a, b in LATE_RUNS:
            gather_pairs(LATE, a, b)
        laid = [lay_tokens(s) for s in range(len(SHARED))]
        for first, last in SCALAR_WEIGHTS:
            round_weights_on_scalar(first, last)
        for g in range(count):
            interleave(g)

        shared_codes = keep.tile([P, T + N], U32, name="shared_codes", tag="picked_1", align_bytes=64)
        codes.extend(shared_codes[:, a:b] for a, b in SHARED)
        for g, (a, b) in enumerate(GROUPS):
            if g == count - 1:
                quantize_weights(E, E + 1, shared_codes[:, T:])
                shared_expert(0, laid[0])
                empty_shared(0)
            made = keep.tile([P, (b - a) // C * N], U32, name="w_codes_%d" % g, align_bytes=64)
            quantize_weights(a // C, b // C, made[:])
            experts(g)

        for s in range(1, len(SHARED)):
            shared_expert(s, laid[s])

        result = keep.tile([P, T], F32, name="result")
        turned = keep.tile([P, T], F32, name="turned")
        relay = keep.tile([P, 2 * SPAN], F32, name="relay", tag="picked_0", align_bytes=64)
        spent = w_raw[GPSIMD_WEIGHTS[2][0]][:].rearrange("p e j n -> p (e j n)")
        sums = {chunk: banks[FIRST_SUM_BANK + c] for c, chunk in enumerate(CHUNKS)}
        backs = {chunk: banks[c] for c, chunk in enumerate(CHUNKS)}
        summands = {chunk: 4 if chunk in WHOLLY_SUMMED else 3 for chunk in CHUNKS}
        added = {chunk: 0 for chunk in CHUNKS}
        blocks = [slice(i, i + P) for i in range(0, CHUNK, P)]

        def add(chunk, term):
            for i, block in enumerate(blocks):
                nc.tensor.matmul(
                    sums[chunk][:, block],
                    term[:, block],
                    identity[:],
                    start=added[chunk] == 0 and i == 0,
                    stop=added[chunk] == summands[chunk] - 1 and i == len(blocks) - 1,
                    is_transpose=True,
                )
            added[chunk] = added[chunk] + 1

        def add_shared(chunk):
            add(chunk, ys[:, chunk[0] : chunk[1]])

        def new_term(r, chunk):
            return keep.tile([P, CHUNK], F32, name="term_%d_%d" % (chunk[0], r))[:]

        def add_fetched(chunk, r):
            add(chunk, fetch_term(r, *chunk, new_term(r, chunk)))

        def add_weighed_in_place(chunk, r, plain):
            add(chunk, weigh(r, *chunk, plain, plain))

        def turn_back(chunk):
            rows = turned[:, chunk[0] : chunk[1]]
            nc.scalar.copy(rows, sums[chunk][:, :CHUNK])
            for block in blocks:
                nc.tensor.transpose(backs[chunk][:, block], rows[:, block], identity[:])

        def store(chunk):
            a, b = chunk
            nc.scalar.copy(result[:, a:b], backs[chunk][:, :CHUNK])
            nc.sync.dma_start(out[:, a:b], result[:, a:b])

        def finish(chunk, term, a, b):
            cols = slice(a - chunk[0], b - chunk[0])
            nc.vector.tensor_tensor(result[:, a:b], backs[chunk][:, cols], term[:, cols], ADD)
            nc.sync.dma_start(out[:, a:b], result[:, a:b])

        add_shared(FIRST)
        add_shared(SECOND)
        empty_shared(1)
        add_shared(THIRD)
        add_shared(FOURTH)
        add_fetched(FIRST, 0)
        add_fetched(FIRST, 1)
        add(FIRST, fetch_term(2, *FIRST, relay[:, RELAY_FIRST_TERM]))
        second_2 = fetch_plain(2, *SECOND, spent[:, :CHUNK])
        third_2 = fetch_plain(2, *THIRD, spent[:, CHUNK : 2 * CHUNK])
        empty_shared(2)
        add_shared(FIFTH)
        third_0 = fetch_plain(0, *THIRD, spent[:, 2 * CHUNK : 3 * CHUNK])
        add_weighed_in_place(SECOND, 2, second_2)
        add_fetched(SECOND, 0)
        add_weighed_in_place(THIRD, 2, third_2)
        turn_back(FIRST)
        fourth_0 = fetch_plain(0, *FOURTH, relay[:, RELAY_TERM_0])
        last_2 = fetch_plain(2, FOURTH[0], FIFTH[1], relay[:, RELAY_TERM_2])
        add_fetched(SECOND, 1)
        add_weighed_in_place(THIRD, 0, third_0)
        add_fetched(FIFTH, 0)
        turn_back(SECOND)
        add_weighed_in_place(FOURTH, 0, fourth_0)
        add(FOURTH, weigh(2, *FOURTH, last_2[:, :CHUNK], new_term(2, FOURTH)))
        add(FIFTH, weigh(2, *FIFTH, last_2[:, CHUNK:], new_term(2, FIFTH)))
        turn_back(THIRD)
        store(FIRST)
        turn_back(FOURTH)
        turn_back(FIFTH)
        store(SECOND)
        middle_1 = fetch_term(1, THIRD[0], FOURTH[1], relay[:, RELAY_LAST_TWO])
        fifth_1 = fetch_term(1, *FIFTH, relay[:, RELAY_LAST_ONE])
        finish(THIRD, middle_1[:, :CHUNK], *THIRD)
        finish(FOURTH, middle_1[:, CHUNK:], *FOURTH)
        finish(FIFTH, fifth_1, FIFTH[0], LAST_CUT)
        finish(FIFTH, fifth_1, LAST_CUT, T)
